import numpy as np
import ml_dtypes


def mxq(x, axis, fmt="e4m3"):
    dtype, down = {"e4m3": (ml_dtypes.float8_e4m3fn, 7), "e5m2": (ml_dtypes.float8_e5m2, 14)}[fmt]
    v = np.moveaxis(np.asarray(x, np.float32).astype(ml_dtypes.bfloat16).astype(np.float64), axis, -1)
    blocks = v.reshape(v.shape[:-1] + (-1, 32))
    amax = np.abs(blocks).max(-1, keepdims=True)
    byte = np.maximum(np.where(amax > 0, np.frexp(amax)[1] - 1 + 127, 0) - down, 1)
    scale = np.exp2(byte - 127.0)
    codes = (blocks / scale).astype(np.float32).astype(dtype).astype(np.float64)
    return np.moveaxis((codes * scale).reshape(v.shape), -1, axis)


WIDE = False


def mx_kscale(k):
    if not WIDE:
        return np.ones(k)
    levels = np.array([10, -10, 5, -5, 0])
    if k % 512:
        return np.exp2(np.random.permutation(np.resize(levels, k // 32))).repeat(32)
    a = np.empty((k // 512, 16))
    for p in range(k // 512):
        a[p, :8] = np.random.permutation(np.resize(levels, 8))
        for g in range(8):
            far = levels[np.abs(levels - a[p, g]) >= 10]
            a[p, g + 8] = far[np.random.randint(len(far))]
    return np.exp2(a.ravel()).repeat(32)


def f64(x):
    return np.asarray(x).astype(np.float64)


def striped(idx):
    return np.tile(idx.reshape(-1, 16).T, (8, 1)).astype(np.uint16)


def unstriped(offs):
    return offs[:16].T.reshape(-1).astype(np.int64)


E2M1 = np.array([0.0, 0.5, 1.0, 1.5, 2.0, 3.0, 4.0, 6.0, -0.0, -0.5, -1.0, -1.5, -2.0, -3.0, -4.0, -6.0])


def pack_weight(w, fmt):
    k, n = w.shape
    w = f64(np.asarray(w, np.float32).astype(ml_dtypes.bfloat16)).reshape(k // 32, 32, n)
    amax = np.abs(w).max(1)
    if fmt == "e4m3":
        byte = np.frexp(amax)[1] - 1 + 127 - 7
    else:
        mant, ex = np.frexp(amax / 6.0)
        byte = np.where(mant > 0.5, ex, ex - 1) + 127
    byte = np.clip(np.where(amax > 0, byte, 1), 1, 254)
    scaled = (w * np.exp2(127.0 - byte)[:, None, :]).reshape(k, n).astype(np.float32)
    by_word = np.ascontiguousarray(scaled.reshape(k // 512, 128, 4, n).transpose(0, 1, 3, 2))
    if fmt == "e4m3":
        words = by_word.astype(ml_dtypes.float8_e4m3fn).view(np.uint8)
    else:
        c = by_word.astype(ml_dtypes.float4_e2m1fn).view(np.uint8) & 0xF
        words = (c[..., 0::2] | (c[..., 1::2] << 4)).reshape(k // 512, 128, 2 * n)
    return np.ascontiguousarray(words), np.ascontiguousarray(byte.astype(np.uint8).reshape(k // 512, 16, n))


def unpack_weight(words, scales, fmt):
    g, _, n = scales.shape
    words = np.ascontiguousarray(words).reshape(g, 128, n, -1)
    if fmt == "e4m3":
        vals = words.view(ml_dtypes.float8_e4m3fn).astype(np.float64)
    else:
        nib = np.empty((g, 128, n, 4), np.uint8)
        nib[..., 0::2] = words & 0xF
        nib[..., 1::2] = words >> 4
        vals = E2M1[nib]
    vals = vals * np.repeat(np.exp2(scales.astype(np.float64) - 127.0), 8, axis=1)[..., None]
    return vals.transpose(0, 1, 3, 2).reshape(g * 512, n)


def silu(v):
    return v / (1.0 + np.exp(-np.maximum(v, -700.0)))


K, T, E, C, H, N = 512, 768, 3, 256, 512, 256


def by_expert(wq, xq):
    return np.concatenate([wq[e].T @ xq[:, e * C:(e + 1) * C] for e in range(E)], axis=1)


def setup_inputs():
    n = np.random.standard_normal
    s = mx_kscale(K)
    u = mx_kscale(H)
    slot_token = np.concatenate([np.random.permutation(T)[:C] for e in range(E)])
    x = pack_weight(n((K, T)) * s[:, None], "e4m3")
    w = [pack_weight(m, "e2m1") for m in n((E, K, N)) / np.sqrt(K) / s[None, :, None]]
    wa = [pack_weight(m, "e4m3") for m in n((E, K, H)) / np.sqrt(K) / s[None, :, None] * u]
    return {
        "x_words": x[0],
        "x_scales": x[1],
        "w_words": np.stack([m[0] for m in w]),
        "w_scales": np.stack([m[1] for m in w]),
        "wa_words": np.stack([m[0] for m in wa]),
        "wa_scales": np.stack([m[1] for m in wa]),
        "wb": (n((E, H, N)) / np.sqrt(H) / u[None, :, None]).astype(np.float32),
        "offs": striped(slot_token),
    }


def reference(x_words, x_scales, w_words, w_scales, wa_words, wa_scales, wb, offs):
    w = np.stack([unpack_weight(w_words[e], w_scales[e], "e2m1") for e in range(E)])
    wa = np.stack([unpack_weight(wa_words[e], wa_scales[e], "e4m3") for e in range(E)])
    wbq = mxq(f64(wb), 1, "e4m3")
    idx = unstriped(offs)
    xq = unpack_weight(x_words, x_scales, "e4m3")[:, idx]
    h = silu(by_expert(wa, xq))
    y = by_expert(w, xq) + by_expert(wbq, mxq(h, 0, "e4m3"))
    out = y
    return out

@@ -1,0 +1,191 @@
+from contextlib import ExitStack
+
+import concourse.mybir as mybir
+
+K, T, E, C, H, N = 512, 768, 3, 256, 512, 256
+FLOPS = 2 * E * C * (K * H + K * N + H * N)
+
+F32 = mybir.dt.float32
+BF16 = mybir.dt.bfloat16
+I32 = mybir.dt.int32
+U32 = mybir.dt.uint32
+U16 = mybir.dt.uint16
+U8 = mybir.dt.uint8
+FP8X4 = mybir.dt.float8_e4m3fn_x4
+FP4X4 = mybir.dt.float4_e2m1fn_x4
+SILU = mybir.ActivationFunctionType.Silu
+
+P = 128
+PACK = 4
+LINE = 4
+M = 128
+HALVES = C // M
+N_TILES = N // M
+COLS = C // 16
+
+
+def load_scale_rows(queue, plane, rows):
+    for r in range(4):
+        queue.dma_start(out=plane[r:P:32], in_=rows[r:16:4])
+
+
+def tile_moe_elr_s_silu_kernel(
+    tc, x_words, x_scales, w_words, w_scales, wa_words, wa_scales, wb, offs, out
+):
+    nc = tc.nc
+    with ExitStack() as ctx:
+        lists = ctx.enter_context(tc.tile_pool(name="lists", bufs=1))
+        keep = ctx.enter_context(tc.tile_pool(name="keep", bufs=1))
+        psum_h = ctx.enter_context(tc.psum_pool(name="psum_h", bufs=4))
+        psum_y = ctx.enter_context(tc.psum_pool(name="psum_y", bufs=4))
+
+        def per_expert(name, shape, dtype):
+            return [keep.tile(shape, dtype, name=f"{name}{e}", align_bytes=64) for e in range(E)]
+
+        offsets = lists.tile([P, T // 16], U16, name="offsets")
+        x_window = keep.tile([P, T], U32, name="x_window", align_bytes=64)
+        xs_window = keep.tile([P, T], U8, name="xs_window", align_bytes=64)
+        was_raw = keep.tile([P, E, H], U8, name="was_raw", align_bytes=64)
+        ws_plane = keep.tile([P, E, N], U8, name="ws_plane", align_bytes=64)
+        w_codes = keep.tile([P, E, 2 * N], U8, name="w_codes", align_bytes=64)
+        warm_in = keep.tile([P, 8], F32, name="warm_in")
+        warm_out = keep.tile([P, 8], F32, name="warm_out")
+        wa_raw = per_expert("wa_raw", [P, H], I32)
+        wa_codes = per_expert("wa_codes", [P, H], I32)
+        wa_plane = per_expert("wa_plane", [P, H], U8)
+        wb_raw = per_expert("wb_raw", [P, PACK, N], F32)
+        wb_bf = per_expert("wb_bf", [P, N, PACK], BF16)
+        wb_codes = per_expert("wb_codes", [P, N], U32)
+        wb_plane = per_expert("wb_plane", [P, N], U8)
+        x_codes = per_expert("x_codes", [P, C], U32)
+        x_plane = per_expert("x_plane", [P, C], U8)
+        h_codes = per_expert("h_codes", [P, C], U32)
+        h_plane = per_expert("h_plane", [P, C], U8)
+        h_bf = per_expert("h_bf", [P, C, PACK], BF16)
+
+        nc.vector.memset(xs_window[:].bitcast(I32), 0)
+        nc.vector.memset(was_raw[:].rearrange("p e i -> p (e i)").bitcast(I32), 0)
+        nc.gpsimd.memset(ws_plane[:].rearrange("p e n -> p (e n)").bitcast(I32), 0)
+        nc.vector.memset(warm_in[:], 0.0)
+
+        def load_wa(e):
+            nc.sync.dma_start(out=wa_raw[e][:], in_=wa_words[e, 0].rearrange("p i d -> p (i d)").bitcast(I32))
+
+        def load_wb(e):
+            nc.sync.dma_start(out=wb_raw[e][:], in_=wb[e].rearrange("(p j) n -> p j n", j=PACK))
+
+        nc.sync.dma_start(offsets[:], offs)
+        nc.sync.dma_start(out=x_window[:].bitcast(I32), in_=x_words[0].rearrange("p t d -> p (t d)").bitcast(I32))
+        load_scale_rows(nc.scalar, xs_window[:].bitcast(I32), x_scales[0].bitcast(I32))
+        load_wa(0)
+        load_wb(0)
+        nc.scalar.activation(warm_out[:], warm_in[:], SILU)
+        load_scale_rows(nc.scalar, was_raw[:].bitcast(I32), wa_scales[:, 0].rearrange("e b i -> b e i").bitcast(I32))
+        load_wa(1)
+        load_wb(1)
+        load_wa(2)
+        load_wb(2)
+        load_scale_rows(nc.sync, ws_plane[:].bitcast(I32), w_scales[:, 0].rearrange("e b n -> b e n").bitcast(I32))
+        nc.sync.dma_start(out=w_codes[:].bitcast(I32), in_=w_words[:, 0].rearrange("e p b -> p e b").bitcast(I32))
+
+        def gather(e):
+            slots = offsets[:, e * COLS : (e + 1) * COLS]
+            nc.vector.tensor_copy(x_codes[e][:], x_window[:].indirect(slots))
+            nc.vector.tensor_copy(x_plane[e][:], xs_window[:].indirect(slots))
+
+        def permute_wa(e):
+            nc.vector.tensor_copy(
+                out=wa_codes[e][:].rearrange("p (t c i) -> p c t i", t=PACK, i=LINE),
+                in_=wa_raw[e][:].rearrange("p (c i t) -> p c t i", t=PACK, i=LINE),
+            )
+            nc.vector.tensor_copy(
+                out=wa_plane[e][:].rearrange("p (t m) -> p t m", t=PACK),
+                in_=was_raw[:, e, :].rearrange("p (m t) -> p t m", t=PACK),
+            )
+
+        def round_wb(e, copy):
+            copy(
+                out=wb_bf[e][:].rearrange("p (c i) j -> p c j i", i=LINE),
+                in_=wb_raw[e][:].rearrange("p j (c i) -> p c j i", i=LINE),
+            )
+
+        def quantize_wb(e):
+            nc.vector.quantize_mx(
+                out=wb_codes[e][:].bitcast(FP8X4),
+                scales=wb_plane[e][:],
+                in_=wb_bf[e][:].rearrange("p n j -> p (n j)"),
+            )
+
+        def hidden(e, s):
+            slots = slice(s * M, (s + 1) * M)
+            acc = psum_h.tile([P, PACK, M], F32, name="h_acc")
+            for t in range(PACK):
+                cols = slice(t * M, (t + 1) * M)
+                nc.tensor.matmul_mx(
+                    out=acc[:, t, :],
+                    lhsT=wa_codes[e][:, cols].bitcast(FP8X4),
+                    lhsT_scale=wa_plane[e][:, cols],
+                    rhs=x_codes[e][:, slots].bitcast(FP8X4),
+                    rhs_scale=x_plane[e][:, slots],
+                    start=True,
+                    stop=True,
+                )
+            nc.scalar.activation(h_bf[e][:, slots, :], acc[:].rearrange("p t u -> p u t"), SILU)
+
+        def quantize_hidden(e, s):
+            slots = slice(s * M, (s + 1) * M)
+            nc.vector.quantize_mx(
+                out=h_codes[e][:, slots].bitcast(FP8X4),
+                scales=h_plane[e][:, slots],
+                in_=h_bf[e][:, slots, :].rearrange("p u t -> p (u t)"),
+            )
+
+        def result(e, b, copy):
+            cols = slice(b * M, (b + 1) * M)
+            acc = psum_y.tile([P, C], F32, name="y_acc")
+            for s in range(HALVES):
+                slots = slice(s * M, (s + 1) * M)
+                nc.tensor.matmul_mx(
+                    out=acc[:, slots],
+                    lhsT=wb_codes[e][:, cols].bitcast(FP8X4),
+                    lhsT_scale=wb_plane[e][:, cols],
+                    rhs=h_codes[e][:, slots].bitcast(FP8X4),
+                    rhs_scale=h_plane[e][:, slots],
+                    start=True,
+                    stop=False,
+                )
+                nc.tensor.matmul_mx(
+                    out=acc[:, slots],
+                    lhsT=w_codes[:, e, 2 * b * M : 2 * (b + 1) * M].bitcast(FP4X4),
+                    lhsT_scale=ws_plane[:, e, cols],
+                    rhs=x_codes[e][:, slots].bitcast(FP8X4),
+                    rhs_scale=x_plane[e][:, slots],
+                    start=False,
+                    stop=True,
+                )
+            y = keep.tile([P, C], F32, name=f"y{e}_{b}")
+            copy(out=y[:], in_=acc[:])
+            nc.sync.dma_start(out=out[cols, e * C : (e + 1) * C], in_=y[:])
+
+        def first_layer(e):
+            gather(e)
+            permute_wa(e)
+            for s in range(HALVES):
+                hidden(e, s)
+
+        def second_layer(e):
+            quantize_wb(e)
+            for s in range(HALVES):
+                quantize_hidden(e, s)
+            result(e, 0, nc.scalar.copy)
+            result(e, 1, nc.vector.tensor_copy)
+
+        round_wb(0, nc.scalar.copy)
+        first_layer(0)
+        round_wb(1, nc.scalar.copy)
+        first_layer(1)
+        second_layer(0)
+        first_layer(2)
+        round_wb(2, nc.vector.tensor_copy)
+        second_layer(1)
+        second_layer(2)

@@ -36,30 +36,30 @@ def tile_moe_elr_s_silu_kernel(
     with ExitStack() as ctx:
         lists = ctx.enter_context(tc.tile_pool(name="lists", bufs=1))
         keep = ctx.enter_context(tc.tile_pool(name="keep", bufs=1))
-        psum_h = ctx.enter_context(tc.psum_pool(name="psum_h", bufs=4))
-        psum_y = ctx.enter_context(tc.psum_pool(name="psum_y", bufs=4))
+        psum_h = ctx.enter_context(tc.psum_pool(name="psum_h", bufs=3))
+        psum_y = ctx.enter_context(tc.psum_pool(name="psum_y", bufs=5))
 
         def per_expert(name, shape, dtype):
-            return [keep.tile(shape, dtype, name=f"{name}{e}", align_bytes=64) for e in range(E)]
+            return [keep.tile(shape, dtype, name=f"{name}{e}", tag=f"{name}{e}", align_bytes=64) for e in range(E)]
 
         offsets = lists.tile([P, T // 16], U16, name="offsets")
         x_window = keep.tile([P, T], U32, name="x_window", align_bytes=64)
         xs_window = keep.tile([P, T], U8, name="xs_window", align_bytes=64)
-        was_raw = keep.tile([P, E, H], U8, name="was_raw", align_bytes=64)
+        was_raw = keep.tile([P, E, H], U8, name="was_raw", tag="was_raw", align_bytes=64)
         ws_plane = keep.tile([P, E, N], U8, name="ws_plane", align_bytes=64)
         w_codes = keep.tile([P, E, 2 * N], U8, name="w_codes", align_bytes=64)
         warm_in = keep.tile([P, 8], F32, name="warm_in")
         warm_out = keep.tile([P, 8], F32, name="warm_out")
         wa_raw = per_expert("wa_raw", [P, H], I32)
         wa_codes = per_expert("wa_codes", [P, H], I32)
-        wa_plane = per_expert("wa_plane", [P, H], U8)
+        wa_plane = keep.tile([P, E, H], U8, name="wa_plane", align_bytes=64)
         wb_raw = per_expert("wb_raw", [P, PACK, N], F32)
-        wb_bf = per_expert("wb_bf", [P, N, PACK], BF16)
-        wb_codes = per_expert("wb_codes", [P, N], U32)
+        wb_bf = {}
         wb_plane = per_expert("wb_plane", [P, N], U8)
-        x_codes = per_expert("x_codes", [P, C], U32)
-        x_plane = per_expert("x_plane", [P, C], U8)
-        h_codes = per_expert("h_codes", [P, C], U32)
+        wb_codes = {}
+        x_codes = {}
+        x_plane = {}
+        h_codes = {}
         h_plane = per_expert("h_plane", [P, C], U8)
         h_bf = per_expert("h_bf", [P, C, PACK], BF16)
 
@@ -74,42 +74,49 @@ def tile_moe_elr_s_silu_kernel(
         def load_wb(e):
             nc.sync.dma_start(out=wb_raw[e][:], in_=wb[e].rearrange("(p j) n -> p j n", j=PACK))
 
+        nc.scalar.activation(warm_out[:], warm_in[:], SILU)
         nc.sync.dma_start(offsets[:], offs)
         nc.sync.dma_start(out=x_window[:].bitcast(I32), in_=x_words[0].rearrange("p t d -> p (t d)").bitcast(I32))
-        load_scale_rows(nc.scalar, xs_window[:].bitcast(I32), x_scales[0].bitcast(I32))
-        load_wa(0)
+        load_scale_rows(nc.sync, xs_window[:].bitcast(I32), x_scales[0].bitcast(I32))
         load_wb(0)
-        nc.scalar.activation(warm_out[:], warm_in[:], SILU)
-        load_scale_rows(nc.scalar, was_raw[:].bitcast(I32), wa_scales[:, 0].rearrange("e b i -> b e i").bitcast(I32))
+        load_wa(0)
+        load_scale_rows(nc.sync, was_raw[:].bitcast(I32), wa_scales[:, 0].rearrange("e b i -> b e i").bitcast(I32))
         load_wa(1)
         load_wb(1)
+        nc.sync.dma_start(out=w_codes[:].bitcast(I32), in_=w_words[:, 0].rearrange("e p b -> p e b").bitcast(I32))
+        load_scale_rows(nc.sync, ws_plane[:].bitcast(I32), w_scales[:, 0].rearrange("e b n -> b e n").bitcast(I32))
         load_wa(2)
         load_wb(2)
-        load_scale_rows(nc.sync, ws_plane[:].bitcast(I32), w_scales[:, 0].rearrange("e b n -> b e n").bitcast(I32))
-        nc.sync.dma_start(out=w_codes[:].bitcast(I32), in_=w_words[:, 0].rearrange("e p b -> p e b").bitcast(I32))
 
-        def gather(e):
-            slots = offsets[:, e * COLS : (e + 1) * COLS]
-            nc.vector.tensor_copy(x_codes[e][:], x_window[:].indirect(slots))
-            nc.vector.tensor_copy(x_plane[e][:], xs_window[:].indirect(slots))
+        def gather_words(e, tag):
+            x_codes[e] = keep.tile([P, C], U32, name=f"x_codes{e}", tag=tag, align_bytes=64)
+            nc.vector.tensor_copy(x_codes[e][:], x_window[:].indirect(offsets[:, e * COLS : (e + 1) * COLS]))
 
-        def permute_wa(e):
+        def gather_scales(e, tag):
+            x_plane[e] = keep.tile([P, C], U8, name=f"x_plane{e}", tag=tag, align_bytes=64)
+            nc.vector.tensor_copy(x_plane[e][:], xs_window[:].indirect(offsets[:, e * COLS : (e + 1) * COLS]))
+
+        def permute_words(e):
             nc.vector.tensor_copy(
                 out=wa_codes[e][:].rearrange("p (t c i) -> p c t i", t=PACK, i=LINE),
                 in_=wa_raw[e][:].rearrange("p (c i t) -> p c t i", t=PACK, i=LINE),
             )
+
+        def permute_scales(experts):
             nc.vector.tensor_copy(
-                out=wa_plane[e][:].rearrange("p (t m) -> p t m", t=PACK),
-                in_=was_raw[:, e, :].rearrange("p (m t) -> p t m", t=PACK),
+                out=wa_plane[:, experts, :].rearrange("p e (t m) -> p e t m", t=PACK),
+                in_=was_raw[:, experts, :].rearrange("p e (m t) -> p e t m", t=PACK),
             )
 
-        def round_wb(e, copy):
+        def round_wb(e, copy, tag):
+            wb_bf[e] = keep.tile([P, N, PACK], BF16, name=f"wb_bf{e}", tag=tag, align_bytes=64)
             copy(
                 out=wb_bf[e][:].rearrange("p (c i) j -> p c j i", i=LINE),
                 in_=wb_raw[e][:].rearrange("p j (c i) -> p c j i", i=LINE),
             )
 
-        def quantize_wb(e):
+        def quantize_wb(e, tag):
+            wb_codes[e] = keep.tile([P, N], U32, name=f"wb_codes{e}", tag=tag, align_bytes=64)
             nc.vector.quantize_mx(
                 out=wb_codes[e][:].bitcast(FP8X4),
                 scales=wb_plane[e][:],
@@ -124,7 +131,7 @@ def tile_moe_elr_s_silu_kernel(
                 nc.tensor.matmul_mx(
                     out=acc[:, t, :],
                     lhsT=wa_codes[e][:, cols].bitcast(FP8X4),
-                    lhsT_scale=wa_plane[e][:, cols],
+                    lhsT_scale=wa_plane[:, e, cols],
                     rhs=x_codes[e][:, slots].bitcast(FP8X4),
                     rhs_scale=x_plane[e][:, slots],
                     start=True,
@@ -132,60 +139,91 @@ def tile_moe_elr_s_silu_kernel(
                 )
             nc.scalar.activation(h_bf[e][:, slots, :], acc[:].rearrange("p t u -> p u t"), SILU)
 
-        def quantize_hidden(e, s):
-            slots = slice(s * M, (s + 1) * M)
+        def quantize_hidden(e, slots):
             nc.vector.quantize_mx(
                 out=h_codes[e][:, slots].bitcast(FP8X4),
                 scales=h_plane[e][:, slots],
                 in_=h_bf[e][:, slots, :].rearrange("p u t -> p (u t)"),
             )
 
-        def result(e, b, copy):
+        def frozen_pass(acc, e, b, slots):
+            nc.tensor.matmul_mx(
+                out=acc,
+                lhsT=w_codes[:, e, 2 * b * M : 2 * (b + 1) * M].bitcast(FP4X4),
+                lhsT_scale=ws_plane[:, e, b * M : (b + 1) * M],
+                rhs=x_codes[e][:, slots].bitcast(FP8X4),
+                rhs_scale=x_plane[e][:, slots],
+                start=True,
+                stop=False,
+            )
+
+        def adapter_pass(acc, e, b, slots):
             cols = slice(b * M, (b + 1) * M)
-            acc = psum_y.tile([P, C], F32, name="y_acc")
+            nc.tensor.matmul_mx(
+                out=acc,
+                lhsT=wb_codes[e][:, cols].bitcast(FP8X4),
+                lhsT_scale=wb_plane[e][:, cols],
+                rhs=h_codes[e][:, slots].bitcast(FP8X4),
+                rhs_scale=h_plane[e][:, slots],
+                start=False,
+                stop=True,
+            )
+
+        def whole_result(e, copy):
+            acc = psum_y.tile([P, N_TILES, C], F32, name="y_acc", tag="y_acc")
             for s in range(HALVES):
                 slots = slice(s * M, (s + 1) * M)
-                nc.tensor.matmul_mx(
-                    out=acc[:, slots],
-                    lhsT=wb_codes[e][:, cols].bitcast(FP8X4),
-                    lhsT_scale=wb_plane[e][:, cols],
-                    rhs=h_codes[e][:, slots].bitcast(FP8X4),
-                    rhs_scale=h_plane[e][:, slots],
-                    start=True,
-                    stop=False,
-                )
-                nc.tensor.matmul_mx(
-                    out=acc[:, slots],
-                    lhsT=w_codes[:, e, 2 * b * M : 2 * (b + 1) * M].bitcast(FP4X4),
-                    lhsT_scale=ws_plane[:, e, cols],
-                    rhs=x_codes[e][:, slots].bitcast(FP8X4),
-                    rhs_scale=x_plane[e][:, slots],
-                    start=False,
-                    stop=True,
-                )
-            y = keep.tile([P, C], F32, name=f"y{e}_{b}")
+                for b in range(N_TILES):
+                    frozen_pass(acc[:, b, slots], e, b, slots)
+                    adapter_pass(acc[:, b, slots], e, b, slots)
+            y = keep.tile([P, N_TILES, C], F32, name=f"y{e}")
             copy(out=y[:], in_=acc[:])
-            nc.sync.dma_start(out=out[cols, e * C : (e + 1) * C], in_=y[:])
+            nc.sync.dma_start(out=out[:, e * C : (e + 1) * C].rearrange("(b p) j -> p b j", p=P), in_=y[:])
+
+        def last_result(e):
+            accs = {}
+            for s in range(HALVES):
+                for b in range(N_TILES):
+                    accs[s, b] = psum_y.tile([P, M], F32, name="y_acc", tag="y_acc")
+                    frozen_pass(accs[s, b][:], e, b, slice(s * M, (s + 1) * M))
+            for s in range(HALVES):
+                slots = slice(s * M, (s + 1) * M)
+                quantize_hidden(e, slots)
+                for b, copy in enumerate((nc.scalar.copy, nc.vector.tensor_copy)):
+                    adapter_pass(accs[s, b][:], e, b, slots)
+                    y = keep.tile([P, M], F32, name=f"y{e}_{s}_{b}")
+                    copy(out=y[:], in_=accs[s, b][:])
+                    nc.sync.dma_start(out=out[b * M : (b + 1) * M, e * C + s * M : e * C + (s + 1) * M], in_=y[:])
 
         def first_layer(e):
-            gather(e)
-            permute_wa(e)
             for s in range(HALVES):
                 hidden(e, s)
 
-        def second_layer(e):
-            quantize_wb(e)
-            for s in range(HALVES):
-                quantize_hidden(e, s)
-            result(e, 0, nc.scalar.copy)
-            result(e, 1, nc.vector.tensor_copy)
-
-        round_wb(0, nc.scalar.copy)
+        round_wb(0, nc.scalar.copy, "wb_bf0")
+        gather_words(0, "x_codes0")
+        gather_scales(0, "x_plane0")
+        gather_words(1, "x_codes1")
+        permute_words(0)
+        permute_scales(slice(0, 1))
         first_layer(0)
-        round_wb(1, nc.scalar.copy)
+        round_wb(1, nc.scalar.copy, "wa_codes0")
+        permute_scales(slice(1, E))
+        gather_scales(1, "was_raw")
+        permute_words(1)
         first_layer(1)
-        second_layer(0)
+        quantize_wb(0, "wa_raw1")
+        gather_scales(2, "wb_bf0")
+        h_codes[0] = keep.tile([P, C], U32, name="h_codes0", align_bytes=64)
+        quantize_hidden(0, slice(0, C))
+        whole_result(0, nc.scalar.copy)
+        gather_words(2, "h_bf0")
+        permute_words(2)
         first_layer(2)
-        round_wb(2, nc.vector.tensor_copy)
-        second_layer(1)
-        second_layer(2)
+        quantize_wb(1, "wb_codes1")
+        h_codes[1] = keep.tile([P, C], U32, name="h_codes1", tag="wa_raw2", align_bytes=64)
+        quantize_hidden(1, slice(0, C))
+        round_wb(2, nc.vector.tensor_copy, "wb_bf2")
+        whole_result(1, nc.scalar.copy)
+        quantize_wb(2, "wb_codes2")
+        h_codes[2] = keep.tile([P, C], U32, name="h_codes2", tag="wb_bf2", align_bytes=64)
+        last_result(2)

@@ -48,8 +48,6 @@ def tile_moe_elr_s_silu_kernel(
         was_raw = keep.tile([P, E, H], U8, name="was_raw", tag="was_raw", align_bytes=64)
         ws_plane = keep.tile([P, E, N], U8, name="ws_plane", align_bytes=64)
         w_codes = keep.tile([P, E, 2 * N], U8, name="w_codes", align_bytes=64)
-        warm_in = keep.tile([P, 8], F32, name="warm_in")
-        warm_out = keep.tile([P, 8], F32, name="warm_out")
         wa_raw = per_expert("wa_raw", [P, H], I32)
         wa_codes = per_expert("wa_codes", [P, H], I32)
         wa_plane = keep.tile([P, E, H], U8, name="wa_plane", align_bytes=64)
@@ -66,7 +64,6 @@ def tile_moe_elr_s_silu_kernel(
         nc.vector.memset(xs_window[:].bitcast(I32), 0)
         nc.vector.memset(was_raw[:].rearrange("p e i -> p (e i)").bitcast(I32), 0)
         nc.gpsimd.memset(ws_plane[:].rearrange("p e n -> p (e n)").bitcast(I32), 0)
-        nc.vector.memset(warm_in[:], 0.0)
 
         def load_wa(e):
             nc.sync.dma_start(out=wa_raw[e][:], in_=wa_words[e, 0].rearrange("p i d -> p (i d)").bitcast(I32))
@@ -74,7 +71,6 @@ def tile_moe_elr_s_silu_kernel(
         def load_wb(e):
             nc.sync.dma_start(out=wb_raw[e][:], in_=wb[e].rearrange("(p j) n -> p j n", j=PACK))
 
-        nc.scalar.activation(warm_out[:], warm_in[:], SILU)
         nc.sync.dma_start(offsets[:], offs)
         nc.sync.dma_start(out=x_window[:].bitcast(I32), in_=x_words[0].rearrange("p t d -> p (t d)").bitcast(I32))
         load_scale_rows(nc.sync, xs_window[:].bitcast(I32), x_scales[0].bitcast(I32))

@@ -22,6 +22,7 @@ M = 128
 HALVES = C // M
 N_TILES = N // M
 COLS = C // 16
+Y_BANKS = 5
 
 
 def load_scale_rows(queue, plane, rows):
@@ -36,8 +37,9 @@ def tile_moe_elr_s_silu_kernel(
     with ExitStack() as ctx:
         lists = ctx.enter_context(tc.tile_pool(name="lists", bufs=1))
         keep = ctx.enter_context(tc.tile_pool(name="keep", bufs=1))
+        shared = ctx.enter_context(tc.tile_pool(name="shared", bufs=1))
         psum_h = ctx.enter_context(tc.psum_pool(name="psum_h", bufs=3))
-        psum_y = ctx.enter_context(tc.psum_pool(name="psum_y", bufs=5))
+        psum_y = ctx.enter_context(tc.psum_pool(name="psum_y", bufs=1))
 
         def per_expert(name, shape, dtype):
             return [keep.tile(shape, dtype, name=f"{name}{e}", tag=f"{name}{e}", align_bytes=64) for e in range(E)]
@@ -48,21 +50,29 @@ def tile_moe_elr_s_silu_kernel(
         was_raw = keep.tile([P, E, H], U8, name="was_raw", tag="was_raw", align_bytes=64)
         ws_plane = keep.tile([P, E, N], U8, name="ws_plane", align_bytes=64)
         w_codes = keep.tile([P, E, 2 * N], U8, name="w_codes", align_bytes=64)
-        wa_raw = per_expert("wa_raw", [P, H], I32)
+        wa_raw = [
+            keep.tile([P, H], I32, name="wa_raw0", align_bytes=64),
+            shared.tile([P, H], I32, name="wa_raw1", align_bytes=64, offset=0),
+            keep.tile([P, H], I32, name="wa_raw2", tag="wa_raw2", align_bytes=64),
+        ]
         wa_codes = per_expert("wa_codes", [P, H], I32)
         wa_plane = keep.tile([P, E, H], U8, name="wa_plane", align_bytes=64)
         wb_raw = per_expert("wb_raw", [P, PACK, N], F32)
-        wb_bf = {}
+        wb_bf = per_expert("wb_bf", [P, N, PACK], BF16)
         wb_plane = per_expert("wb_plane", [P, N], U8)
         wb_codes = {}
         x_codes = {}
         x_plane = {}
-        h_codes = {}
+        h_codes = per_expert("h_codes", [P, C], U32)
         h_plane = per_expert("h_plane", [P, C], U8)
-        h_bf = per_expert("h_bf", [P, C, PACK], BF16)
+        h_bf = {e: keep.tile([P, C, PACK], BF16, name=f"h_bf{e}", align_bytes=64) for e in range(1, E)}
 
         nc.vector.memset(xs_window[:].bitcast(I32), 0)
         nc.vector.memset(was_raw[:].rearrange("p e i -> p (e i)").bitcast(I32), 0)
+        warm_in = keep.tile([P, 1], F32, name="warm_in")
+        warm_out = keep.tile([P, 1], F32, name="warm_out")
+        nc.gpsimd.memset(warm_in[:], 0.0)
+        nc.scalar.activation(warm_out[:], warm_in[:], SILU)
         nc.gpsimd.memset(ws_plane[:].rearrange("p e n -> p (e n)").bitcast(I32), 0)
 
         def load_wa(e):
@@ -71,26 +81,30 @@ def tile_moe_elr_s_silu_kernel(
         def load_wb(e):
             nc.sync.dma_start(out=wb_raw[e][:], in_=wb[e].rearrange("(p j) n -> p j n", j=PACK))
 
+        def load_w():
+            nc.sync.dma_start(out=w_codes[:].bitcast(I32), in_=w_words[:, 0].rearrange("e p b -> p e b").bitcast(I32))
+
+        def load_was(queue):
+            load_scale_rows(queue, was_raw[:].bitcast(I32), wa_scales[:, 0].rearrange("e b i -> b e i").bitcast(I32))
+
+        def load_ws(queue):
+            load_scale_rows(queue, ws_plane[:].bitcast(I32), w_scales[:, 0].rearrange("e b n -> b e n").bitcast(I32))
+
         nc.sync.dma_start(offsets[:], offs)
         nc.sync.dma_start(out=x_window[:].bitcast(I32), in_=x_words[0].rearrange("p t d -> p (t d)").bitcast(I32))
         load_scale_rows(nc.sync, xs_window[:].bitcast(I32), x_scales[0].bitcast(I32))
         load_wb(0)
         load_wa(0)
-        load_scale_rows(nc.sync, was_raw[:].bitcast(I32), wa_scales[:, 0].rearrange("e b i -> b e i").bitcast(I32))
-        load_wa(1)
+        load_was(nc.sync)
         load_wb(1)
-        nc.sync.dma_start(out=w_codes[:].bitcast(I32), in_=w_words[:, 0].rearrange("e p b -> p e b").bitcast(I32))
-        load_scale_rows(nc.sync, ws_plane[:].bitcast(I32), w_scales[:, 0].rearrange("e b n -> b e n").bitcast(I32))
+        load_wa(1)
         load_wa(2)
+        load_w()
         load_wb(2)
+        load_ws(nc.sync)
 
-        def gather_words(e, tag):
-            x_codes[e] = keep.tile([P, C], U32, name=f"x_codes{e}", tag=tag, align_bytes=64)
-            nc.vector.tensor_copy(x_codes[e][:], x_window[:].indirect(offsets[:, e * COLS : (e + 1) * COLS]))
-
-        def gather_scales(e, tag):
-            x_plane[e] = keep.tile([P, C], U8, name=f"x_plane{e}", tag=tag, align_bytes=64)
-            nc.vector.tensor_copy(x_plane[e][:], xs_window[:].indirect(offsets[:, e * COLS : (e + 1) * COLS]))
+        def gather(tile, window, first, count):
+            nc.vector.tensor_copy(tile[:], window[:].indirect(offsets[:, first * COLS : (first + count) * COLS]))
 
         def permute_words(e):
             nc.vector.tensor_copy(
@@ -100,12 +114,11 @@ def tile_moe_elr_s_silu_kernel(
 
         def permute_scales(experts):
             nc.vector.tensor_copy(
-                out=wa_plane[:, experts, :].rearrange("p e (t m) -> p e t m", t=PACK),
-                in_=was_raw[:, experts, :].rearrange("p e (m t) -> p e t m", t=PACK),
+                out=wa_plane[:, experts, :].rearrange("p e (t h m) -> p h e t m", t=PACK, h=2),
+                in_=was_raw[:, experts, :].rearrange("p e (h m t) -> p h e t m", t=PACK, h=2),
             )
 
-        def round_wb(e, copy, tag):
-            wb_bf[e] = keep.tile([P, N, PACK], BF16, name=f"wb_bf{e}", tag=tag, align_bytes=64)
+        def round_wb(e, copy):
             copy(
                 out=wb_bf[e][:].rearrange("p (c i) j -> p c j i", i=LINE),
                 in_=wb_raw[e][:].rearrange("p j (c i) -> p c j i", i=LINE),
@@ -166,7 +179,7 @@ def tile_moe_elr_s_silu_kernel(
             )
 
         def whole_result(e, copy):
-            acc = psum_y.tile([P, N_TILES, C], F32, name="y_acc", tag="y_acc")
+            acc = psum_y.tile([P, N_TILES, C], F32, name="y_acc", tag=f"bank{e}")
             for s in range(HALVES):
                 slots = slice(s * M, (s + 1) * M)
                 for b in range(N_TILES):
@@ -176,50 +189,56 @@ def tile_moe_elr_s_silu_kernel(
             copy(out=y[:], in_=acc[:])
             nc.sync.dma_start(out=out[:, e * C : (e + 1) * C].rearrange("(b p) j -> p b j", p=P), in_=y[:])
 
-        def last_result(e):
+        def last_result(e, copies):
             accs = {}
             for s in range(HALVES):
                 for b in range(N_TILES):
-                    accs[s, b] = psum_y.tile([P, M], F32, name="y_acc", tag="y_acc")
+                    bank = (E - 1 + N_TILES * s + b) % Y_BANKS
+                    accs[s, b] = psum_y.tile([P, M], F32, name="y_part", tag=f"bank{bank}")
                     frozen_pass(accs[s, b][:], e, b, slice(s * M, (s + 1) * M))
             for s in range(HALVES):
                 slots = slice(s * M, (s + 1) * M)
-                quantize_hidden(e, slots)
-                for b, copy in enumerate((nc.scalar.copy, nc.vector.tensor_copy)):
+                y = keep.tile([P, N_TILES, M], F32, name=f"y{e}_{s}")
+                for b in range(N_TILES):
                     adapter_pass(accs[s, b][:], e, b, slots)
-                    y = keep.tile([P, M], F32, name=f"y{e}_{s}_{b}")
-                    copy(out=y[:], in_=accs[s, b][:])
-                    nc.sync.dma_start(out=out[b * M : (b + 1) * M, e * C + s * M : e * C + (s + 1) * M], in_=y[:])
+                    copies[s][b](out=y[:, b, :], in_=accs[s, b][:])
+                first = e * C + s * M
+                nc.sync.dma_start(out=out[:, first : first + M].rearrange("(b p) j -> p b j", p=P), in_=y[:])
 
         def first_layer(e):
             for s in range(HALVES):
                 hidden(e, s)
 
-        round_wb(0, nc.scalar.copy, "wb_bf0")
-        gather_words(0, "x_codes0")
-        gather_scales(0, "x_plane0")
-        gather_words(1, "x_codes1")
+        codes01 = keep.tile([P, 2 * C], U32, name="codes01", align_bytes=64)
+        plane01 = keep.tile([P, 2 * C], U8, name="plane01", align_bytes=64)
+        gather(codes01, x_window, 0, 2)
+        gather(plane01, xs_window, 0, 2)
+        for e in range(2):
+            x_codes[e] = codes01[:, e * C : (e + 1) * C]
+            x_plane[e] = plane01[:, e * C : (e + 1) * C]
+        round_wb(0, nc.scalar.copy)
         permute_words(0)
         permute_scales(slice(0, 1))
-        first_layer(0)
-        round_wb(1, nc.scalar.copy, "wa_codes0")
         permute_scales(slice(1, E))
-        gather_scales(1, "was_raw")
+        round_wb(1, nc.scalar.copy)
+        h_bf[0] = keep.tile([P, C, PACK], BF16, name="h_bf0", tag="wb_raw1", align_bytes=64)
+        first_layer(0)
         permute_words(1)
         first_layer(1)
-        quantize_wb(0, "wa_raw1")
-        gather_scales(2, "wb_bf0")
-        h_codes[0] = keep.tile([P, C], U32, name="h_codes0", align_bytes=64)
-        quantize_hidden(0, slice(0, C))
-        whole_result(0, nc.scalar.copy)
-        gather_words(2, "h_bf0")
+        x_codes[2] = shared.tile([P, C], U32, name="codes2", align_bytes=64, offset=0)
+        x_plane[2] = shared.tile([P, C], U8, name="plane2", align_bytes=64, offset=4 * C)
+        gather(x_codes[2], x_window, 2, 1)
+        gather(x_plane[2], xs_window, 2, 1)
         permute_words(2)
         first_layer(2)
+        quantize_hidden(0, slice(0, C))
+        quantize_wb(0, "wa_raw2")
         quantize_wb(1, "wb_codes1")
-        h_codes[1] = keep.tile([P, C], U32, name="h_codes1", tag="wa_raw2", align_bytes=64)
+        whole_result(0, nc.scalar.copy)
         quantize_hidden(1, slice(0, C))
-        round_wb(2, nc.vector.tensor_copy, "wb_bf2")
         whole_result(1, nc.scalar.copy)
+        round_wb(2, nc.vector.tensor_copy)
+        quantize_hidden(2, slice(0, M))
         quantize_wb(2, "wb_codes2")
-        h_codes[2] = keep.tile([P, C], U32, name="h_codes2", tag="wb_bf2", align_bytes=64)
-        last_result(2)
+        quantize_hidden(2, slice(M, C))
+        last_result(2, ((nc.vector.tensor_copy, nc.vector.tensor_copy), (nc.vector.tensor_copy, nc.scalar.copy)))

@@ -22,7 +22,9 @@ M = 128
 HALVES = C // M
 N_TILES = N // M
 COLS = C // 16
-Y_BANKS = 5
+WAS_AT = 0
+WA_AT = 2048
+WB_AT = WA_AT + E * 4 * H
 
 
 def load_scale_rows(queue, plane, rows):
@@ -38,7 +40,7 @@ def tile_moe_elr_s_silu_kernel(
         lists = ctx.enter_context(tc.tile_pool(name="lists", bufs=1))
         keep = ctx.enter_context(tc.tile_pool(name="keep", bufs=1))
         shared = ctx.enter_context(tc.tile_pool(name="shared", bufs=1))
-        psum_h = ctx.enter_context(tc.psum_pool(name="psum_h", bufs=3))
+        psum_h = ctx.enter_context(tc.psum_pool(name="psum_h", bufs=4))
         psum_y = ctx.enter_context(tc.psum_pool(name="psum_y", bufs=1))
 
         def per_expert(name, shape, dtype):
@@ -47,25 +49,32 @@ def tile_moe_elr_s_silu_kernel(
         offsets = lists.tile([P, T // 16], U16, name="offsets")
         x_window = keep.tile([P, T], U32, name="x_window", align_bytes=64)
         xs_window = keep.tile([P, T], U8, name="xs_window", align_bytes=64)
-        was_raw = keep.tile([P, E, H], U8, name="was_raw", tag="was_raw", align_bytes=64)
+        def placed(name, shape, dtype, offset):
+            return shared.tile(shape, dtype, name=name, align_bytes=64, offset=offset)
+
+        was_raw = placed("was_raw", [P, E, H], U8, WAS_AT)
+        wa_raw = [placed(f"wa_raw{e}", [P, H], I32, WA_AT + e * 4 * H) for e in range(E)]
+        wb_raw = [placed(f"wb_raw{e}", [P, PACK, N], F32, WB_AT + e * 4 * PACK * N) for e in range(E)]
         ws_plane = keep.tile([P, E, N], U8, name="ws_plane", align_bytes=64)
         w_codes = keep.tile([P, E, 2 * N], U8, name="w_codes", align_bytes=64)
-        wa_raw = [
-            keep.tile([P, H], I32, name="wa_raw0", align_bytes=64),
-            shared.tile([P, H], I32, name="wa_raw1", align_bytes=64, offset=0),
-            keep.tile([P, H], I32, name="wa_raw2", tag="wa_raw2", align_bytes=64),
-        ]
         wa_codes = per_expert("wa_codes", [P, H], I32)
         wa_plane = keep.tile([P, E, H], U8, name="wa_plane", align_bytes=64)
-        wb_raw = per_expert("wb_raw", [P, PACK, N], F32)
         wb_bf = per_expert("wb_bf", [P, N, PACK], BF16)
         wb_plane = per_expert("wb_plane", [P, N], U8)
+        h_plane = per_expert("h_plane", [P, C], U8)
         wb_codes = {}
         x_codes = {}
         x_plane = {}
-        h_codes = per_expert("h_codes", [P, C], U32)
-        h_plane = per_expert("h_plane", [P, C], U8)
-        h_bf = {e: keep.tile([P, C, PACK], BF16, name=f"h_bf{e}", align_bytes=64) for e in range(1, E)}
+        h_codes = {}
+        h_bf = {}
+        h_in = {}
+
+        def made(name, shape, dtype, at):
+            if at is None:
+                return keep.tile(shape, dtype, name=name, align_bytes=64)
+            if isinstance(at, str):
+                return keep.tile(shape, dtype, name=name, tag=at, align_bytes=64)
+            return placed(name, shape, dtype, at)
 
         nc.vector.memset(xs_window[:].bitcast(I32), 0)
         nc.vector.memset(was_raw[:].rearrange("p e i -> p (e i)").bitcast(I32), 0)
@@ -103,8 +112,20 @@ def tile_moe_elr_s_silu_kernel(
         load_wb(2)
         load_ws(nc.sync)
 
-        def gather(tile, window, first, count):
+        def gather(into, window, dtype, name, first, count, at):
+            tile = made(f"{name}{first}", [P, count * C], dtype, at)
             nc.vector.tensor_copy(tile[:], window[:].indirect(offsets[:, first * COLS : (first + count) * COLS]))
+            for e in range(count):
+                into[first + e] = tile[:, e * C : (e + 1) * C]
+
+        def gather_words(first, count, at):
+            gather(x_codes, x_window, U32, "x_codes", first, count, at)
+
+        def gather_scales(first, count, at):
+            gather(x_plane, xs_window, U8, "x_plane", first, count, at)
+
+        def hidden_codes(e, at):
+            h_codes[e] = made(f"h_codes{e}", [P, C], U32, at)
 
         def permute_words(e):
             nc.vector.tensor_copy(
@@ -124,8 +145,8 @@ def tile_moe_elr_s_silu_kernel(
                 in_=wb_raw[e][:].rearrange("p j (c i) -> p c j i", i=LINE),
             )
 
-        def quantize_wb(e, tag):
-            wb_codes[e] = keep.tile([P, N], U32, name=f"wb_codes{e}", tag=tag, align_bytes=64)
+        def quantize_wb(e, at):
+            wb_codes[e] = made(f"wb_codes{e}", [P, N], U32, at)
             nc.vector.quantize_mx(
                 out=wb_codes[e][:].bitcast(FP8X4),
                 scales=wb_plane[e][:],
@@ -146,99 +167,96 @@ def tile_moe_elr_s_silu_kernel(
                     start=True,
                     stop=True,
                 )
-            nc.scalar.activation(h_bf[e][:, slots, :], acc[:].rearrange("p t u -> p u t"), SILU)
+            nc.scalar.activation(h_bf[e, s], acc[:].rearrange("p t u -> p u t"), SILU)
 
         def quantize_hidden(e, slots):
             nc.vector.quantize_mx(
                 out=h_codes[e][:, slots].bitcast(FP8X4),
                 scales=h_plane[e][:, slots],
-                in_=h_bf[e][:, slots, :].rearrange("p u t -> p (u t)"),
+                in_=h_in[e, slots.start].rearrange("p u t -> p (u t)"),
             )
 
-        def frozen_pass(acc, e, b, slots):
-            nc.tensor.matmul_mx(
-                out=acc,
-                lhsT=w_codes[:, e, 2 * b * M : 2 * (b + 1) * M].bitcast(FP4X4),
-                lhsT_scale=ws_plane[:, e, b * M : (b + 1) * M],
-                rhs=x_codes[e][:, slots].bitcast(FP8X4),
-                rhs_scale=x_plane[e][:, slots],
-                start=True,
-                stop=False,
-            )
+        sums = {}
 
-        def adapter_pass(acc, e, b, slots):
-            cols = slice(b * M, (b + 1) * M)
-            nc.tensor.matmul_mx(
-                out=acc,
-                lhsT=wb_codes[e][:, cols].bitcast(FP8X4),
-                lhsT_scale=wb_plane[e][:, cols],
-                rhs=h_codes[e][:, slots].bitcast(FP8X4),
-                rhs_scale=h_plane[e][:, slots],
-                start=False,
-                stop=True,
-            )
+        def frozen_layer(e, first, width):
+            acc = psum_y.tile([P, N_TILES, width], F32, name="y_acc", tag=f"y{e}_{first}")
+            sums[e, first] = acc
+            for b in range(N_TILES):
+                for s in range(0, width, M):
+                    slots = slice(first + s, first + s + M)
+                    nc.tensor.matmul_mx(
+                        out=acc[:, b, s : s + M],
+                        lhsT=w_codes[:, e, 2 * b * M : 2 * (b + 1) * M].bitcast(FP4X4),
+                        lhsT_scale=ws_plane[:, e, b * M : (b + 1) * M],
+                        rhs=x_codes[e][:, slots].bitcast(FP8X4),
+                        rhs_scale=x_plane[e][:, slots],
+                        start=(b == 0 and s == 0),
+                        stop=False,
+                    )
 
-        def whole_result(e, copy):
-            acc = psum_y.tile([P, N_TILES, C], F32, name="y_acc", tag=f"bank{e}")
-            for s in range(HALVES):
-                slots = slice(s * M, (s + 1) * M)
-                for b in range(N_TILES):
-                    frozen_pass(acc[:, b, slots], e, b, slots)
-                    adapter_pass(acc[:, b, slots], e, b, slots)
-            y = keep.tile([P, N_TILES, C], F32, name=f"y{e}")
+        def second_layer(e, first, width, copy, queue=nc.sync):
+            acc = sums[e, first]
+            slots = slice(first, first + width)
+            for b in range(N_TILES):
+                cols = slice(b * M, (b + 1) * M)
+                nc.tensor.matmul_mx(
+                    out=acc[:, b, :],
+                    lhsT=wb_codes[e][:, cols].bitcast(FP8X4),
+                    lhsT_scale=wb_plane[e][:, cols],
+                    rhs=h_codes[e][:, slots].bitcast(FP8X4),
+                    rhs_scale=h_plane[e][:, slots],
+                    start=False,
+                    stop=(b == N_TILES - 1),
+                )
+            y = keep.tile([P, N_TILES, width], F32, name=f"y{e}_{first}")
             copy(out=y[:], in_=acc[:])
-            nc.sync.dma_start(out=out[:, e * C : (e + 1) * C].rearrange("(b p) j -> p b j", p=P), in_=y[:])
+            columns = out[:, e * C + first : e * C + first + width]
+            queue.dma_start(out=columns.rearrange("(b p) j -> p b j", p=P), in_=y[:])
 
-        def last_result(e, copies):
-            accs = {}
+        def first_layer(e, at):
+            tile = made(f"h_bf{e}", [P, C, PACK], BF16, at)
+            h_in[e, 0] = tile[:]
             for s in range(HALVES):
-                for b in range(N_TILES):
-                    bank = (E - 1 + N_TILES * s + b) % Y_BANKS
-                    accs[s, b] = psum_y.tile([P, M], F32, name="y_part", tag=f"bank{bank}")
-                    frozen_pass(accs[s, b][:], e, b, slice(s * M, (s + 1) * M))
-            for s in range(HALVES):
-                slots = slice(s * M, (s + 1) * M)
-                y = keep.tile([P, N_TILES, M], F32, name=f"y{e}_{s}")
-                for b in range(N_TILES):
-                    adapter_pass(accs[s, b][:], e, b, slots)
-                    copies[s][b](out=y[:, b, :], in_=accs[s, b][:])
-                first = e * C + s * M
-                nc.sync.dma_start(out=out[:, first : first + M].rearrange("(b p) j -> p b j", p=P), in_=y[:])
-
-        def first_layer(e):
-            for s in range(HALVES):
+                h_bf[e, s] = tile[:, s * M : (s + 1) * M, :]
                 hidden(e, s)
 
-        codes01 = keep.tile([P, 2 * C], U32, name="codes01", align_bytes=64)
-        plane01 = keep.tile([P, 2 * C], U8, name="plane01", align_bytes=64)
-        gather(codes01, x_window, 0, 2)
-        gather(plane01, xs_window, 0, 2)
-        for e in range(2):
-            x_codes[e] = codes01[:, e * C : (e + 1) * C]
-            x_plane[e] = plane01[:, e * C : (e + 1) * C]
+        def first_layer_half(e, s, at):
+            tile = made(f"h_bf{e}_{s}", [P, M, PACK], BF16, at)
+            h_in[e, s * M] = tile[:]
+            h_bf[e, s] = tile[:]
+            hidden(e, s)
+
+        gather_words(0, 2, "x_pair")
+        gather_scales(0, 2, None)
         round_wb(0, nc.scalar.copy)
         permute_words(0)
         permute_scales(slice(0, 1))
         permute_scales(slice(1, E))
         round_wb(1, nc.scalar.copy)
-        h_bf[0] = keep.tile([P, C, PACK], BF16, name="h_bf0", tag="wb_raw1", align_bytes=64)
-        first_layer(0)
+        first_layer(0, WB_AT + 4 * PACK * N)
         permute_words(1)
-        first_layer(1)
-        x_codes[2] = shared.tile([P, C], U32, name="codes2", align_bytes=64, offset=0)
-        x_plane[2] = shared.tile([P, C], U8, name="plane2", align_bytes=64, offset=4 * C)
-        gather(x_codes[2], x_window, 2, 1)
-        gather(x_plane[2], xs_window, 2, 1)
+        first_layer(1, None)
+        gather_words(2, 1, WA_AT + 4 * H)
+        gather_scales(2, 1, WA_AT + 4 * H + 4 * C)
         permute_words(2)
-        first_layer(2)
+        first_layer_half(2, 0, None)
+        frozen_layer(0, 0, C)
+        hidden_codes(0, None)
         quantize_hidden(0, slice(0, C))
-        quantize_wb(0, "wa_raw2")
-        quantize_wb(1, "wb_codes1")
-        whole_result(0, nc.scalar.copy)
+        quantize_wb(0, WA_AT + 8 * H)
+        quantize_wb(1, None)
+        second_layer(0, 0, C, nc.scalar.copy)
+        frozen_layer(1, 0, C)
+        first_layer_half(2, 1, "x_pair")
+        frozen_layer(2, 0, M)
+        frozen_layer(2, M, M)
+        hidden_codes(1, None)
         quantize_hidden(1, slice(0, C))
-        whole_result(1, nc.scalar.copy)
+        second_layer(1, 0, C, nc.scalar.copy)
         round_wb(2, nc.vector.tensor_copy)
+        hidden_codes(2, None)
         quantize_hidden(2, slice(0, M))
-        quantize_wb(2, "wb_codes2")
+        quantize_wb(2, None)
         quantize_hidden(2, slice(M, C))
-        last_result(2, ((nc.vector.tensor_copy, nc.vector.tensor_copy), (nc.vector.tensor_copy, nc.scalar.copy)))
+        second_layer(2, 0, M, nc.vector.tensor_copy)
+        second_layer(2, M, M, nc.vector.tensor_copy)

@@ -90,6 +90,10 @@ def tile_moe_elr_s_silu_kernel(
         def load_wb(e):
             nc.sync.dma_start(out=wb_raw[e][:], in_=wb[e].rearrange("(p j) n -> p j n", j=PACK))
 
+        def load_wb_rows(e, first):
+            rows = wb[e].rearrange("(p j) n -> p j n", j=PACK)
+            nc.sync.dma_start(out=wb_raw[e][:, first : first + 2, :], in_=rows[:, first : first + 2, :])
+
         def load_w():
             nc.sync.dma_start(out=w_codes[:].bitcast(I32), in_=w_words[:, 0].rearrange("e p b -> p e b").bitcast(I32))
 
@@ -104,8 +108,9 @@ def tile_moe_elr_s_silu_kernel(
         load_scale_rows(nc.sync, xs_window[:].bitcast(I32), x_scales[0].bitcast(I32))
         load_wb(0)
         load_wa(0)
+        load_wb_rows(1, 0)
         load_was(nc.sync)
-        load_wb(1)
+        load_wb_rows(1, 2)
         load_wa(1)
         load_wa(2)
         load_w()
@@ -226,7 +231,7 @@ def tile_moe_elr_s_silu_kernel(
             h_bf[e, s] = tile[:]
             hidden(e, s)
 
-        gather_words(0, 2, "x_pair")
+        gather_words(0, 2, None)
         gather_scales(0, 2, None)
         round_wb(0, nc.scalar.copy)
         permute_words(0)
@@ -236,27 +241,27 @@ def tile_moe_elr_s_silu_kernel(
         first_layer(0, WB_AT + 4 * PACK * N)
         permute_words(1)
         first_layer(1, None)
-        gather_words(2, 1, WA_AT + 4 * H)
-        gather_scales(2, 1, WA_AT + 4 * H + 4 * C)
+        gather_words(2, 1, WB_AT + 6 * PACK * N)
+        gather_scales(2, 1, WB_AT + 7 * PACK * N)
         permute_words(2)
         first_layer_half(2, 0, None)
+        first_layer_half(2, 1, None)
         frozen_layer(0, 0, C)
-        hidden_codes(0, None)
+        hidden_codes(0, "h_codes0")
         quantize_hidden(0, slice(0, C))
-        quantize_wb(0, WA_AT + 8 * H)
+        quantize_wb(0, "wa_codes1")
         quantize_wb(1, None)
-        second_layer(0, 0, C, nc.scalar.copy)
-        frozen_layer(1, 0, C)
-        first_layer_half(2, 1, "x_pair")
-        frozen_layer(2, 0, M)
-        frozen_layer(2, M, M)
+        round_wb(2, nc.vector.tensor_copy)
         hidden_codes(1, None)
         quantize_hidden(1, slice(0, C))
+        second_layer(0, 0, C, nc.vector.tensor_copy)
+        frozen_layer(1, 0, C)
         second_layer(1, 0, C, nc.scalar.copy)
-        round_wb(2, nc.vector.tensor_copy)
-        hidden_codes(2, None)
+        frozen_layer(2, 0, M)
+        frozen_layer(2, M, M)
+        quantize_wb(2, "wa_codes1")
+        hidden_codes(2, "h_codes0")
         quantize_hidden(2, slice(0, M))
-        quantize_wb(2, None)
         quantize_hidden(2, slice(M, C))
-        second_layer(2, 0, M, nc.vector.tensor_copy)
+        second_layer(2, 0, M, nc.scalar.copy)
         second_layer(2, M, M, nc.vector.tensor_copy)

@@ -103,16 +103,21 @@ def tile_moe_elr_s_silu_kernel(
         def load_ws(queue):
             load_scale_rows(queue, ws_plane[:].bitcast(I32), w_scales[:, 0].rearrange("e b n -> b e n").bitcast(I32))
 
+        def load_x():
+            nc.sync.dma_start(out=x_window[:].bitcast(I32), in_=x_words[0].rearrange("p t d -> p (t d)").bitcast(I32))
+
+        def load_xs(queue):
+            load_scale_rows(queue, xs_window[:].bitcast(I32), x_scales[0].bitcast(I32))
+
         nc.sync.dma_start(offsets[:], offs)
-        nc.sync.dma_start(out=x_window[:].bitcast(I32), in_=x_words[0].rearrange("p t d -> p (t d)").bitcast(I32))
-        load_scale_rows(nc.sync, xs_window[:].bitcast(I32), x_scales[0].bitcast(I32))
+        load_x()
+        load_xs(nc.sync)
         load_wb(0)
         load_wa(0)
-        load_wb_rows(1, 0)
-        load_was(nc.sync)
-        load_wb_rows(1, 2)
         load_wa(1)
+        load_was(nc.sync)
         load_wa(2)
+        load_wb(1)
         load_w()
         load_wb(2)
         load_ws(nc.sync)
@@ -235,33 +240,33 @@ def tile_moe_elr_s_silu_kernel(
         gather_scales(0, 2, None)
         round_wb(0, nc.scalar.copy)
         permute_words(0)
+        permute_words(1)
         permute_scales(slice(0, 1))
         permute_scales(slice(1, E))
-        round_wb(1, nc.scalar.copy)
-        first_layer(0, WB_AT + 4 * PACK * N)
-        permute_words(1)
+        first_layer(0, None)
         first_layer(1, None)
-        gather_words(2, 1, WB_AT + 6 * PACK * N)
-        gather_scales(2, 1, WB_AT + 7 * PACK * N)
+        gather_words(2, 1, WAS_AT)
+        gather_scales(2, 1, WAS_AT + 1024)
         permute_words(2)
         first_layer_half(2, 0, None)
         first_layer_half(2, 1, None)
         frozen_layer(0, 0, C)
-        hidden_codes(0, "h_codes0")
+        quantize_wb(0, WA_AT + 2 * 4 * H)
+        hidden_codes(0, WA_AT + 2 * 4 * H + 1024)
         quantize_hidden(0, slice(0, C))
-        quantize_wb(0, "wa_codes1")
+        round_wb(1, nc.vector.tensor_copy)
+        second_layer(0, 0, C, nc.scalar.copy)
+        hidden_codes(1, WB_AT + 4 * PACK * N)
+        quantize_hidden(1, slice(0, C))
         quantize_wb(1, None)
         round_wb(2, nc.vector.tensor_copy)
-        hidden_codes(1, None)
-        quantize_hidden(1, slice(0, C))
-        second_layer(0, 0, C, nc.vector.tensor_copy)
         frozen_layer(1, 0, C)
         second_layer(1, 0, C, nc.scalar.copy)
         frozen_layer(2, 0, M)
         frozen_layer(2, M, M)
-        quantize_wb(2, "wa_codes1")
-        hidden_codes(2, "h_codes0")
+        hidden_codes(2, WB_AT + 8 * PACK * N)
         quantize_hidden(2, slice(0, M))
+        quantize_wb(2, None)
         quantize_hidden(2, slice(M, C))
         second_layer(2, 0, M, nc.scalar.copy)
         second_layer(2, M, M, nc.vector.tensor_copy)

@@ -13,6 +13,7 @@ U16 = mybir.dt.uint16
 U8 = mybir.dt.uint8
 FP8X4 = mybir.dt.float8_e4m3fn_x4
 FP4X4 = mybir.dt.float4_e2m1fn_x4
+ALU = mybir.AluOpType
 SILU = mybir.ActivationFunctionType.Silu
 
 P = 128
@@ -59,7 +60,7 @@ def tile_moe_elr_s_silu_kernel(
         w_codes = keep.tile([P, E, 2 * N], U8, name="w_codes", align_bytes=64)
         wa_codes = per_expert("wa_codes", [P, H], I32)
         wa_plane = keep.tile([P, E, H], U8, name="wa_plane", align_bytes=64)
-        wb_bf = per_expert("wb_bf", [P, N, PACK], BF16)
+        wb_bf = {}
         wb_plane = per_expert("wb_plane", [P, N], U8)
         h_plane = per_expert("h_plane", [P, C], U8)
         wb_codes = {}
@@ -112,14 +113,14 @@ def tile_moe_elr_s_silu_kernel(
         nc.sync.dma_start(offsets[:], offs)
         load_x()
         load_xs(nc.sync)
-        load_wb(0)
         load_wa(0)
         load_wa(1)
+        load_wb(0)
         load_was(nc.sync)
         load_wa(2)
         load_wb(1)
-        load_w()
         load_wb(2)
+        load_w()
         load_ws(nc.sync)
 
         def gather(into, window, dtype, name, first, count, at):
@@ -149,10 +150,33 @@ def tile_moe_elr_s_silu_kernel(
                 in_=was_raw[:, experts, :].rearrange("p e (h m t) -> p h e t m", t=PACK, h=2),
             )
 
-        def round_wb(e, copy):
+        def round_wb(e, copy, at=None):
+            wb_bf[e] = made(f"wb_bf{e}", [P, N, PACK], BF16, at)
             copy(
                 out=wb_bf[e][:].rearrange("p (c i) j -> p c j i", i=LINE),
                 in_=wb_raw[e][:].rearrange("p j (c i) -> p c j i", i=LINE),
+            )
+
+        def round_wb_pool(e, at):
+            wb_bf[e] = made(f"wb_bf{e}", [P, N, PACK], BF16, at)
+            nc.gpsimd.tensor_scalar(
+                wb_bf[e][:], wb_raw[e][:].rearrange("p j n -> p n j"), 1.0, 0.0, op0=ALU.mult, op1=ALU.add
+            )
+
+        def round_block(e, b, copy, at=None):
+            wb_bf[e, b] = made(f"wb_bf{e}_{b}", [P, M, PACK], BF16, at)
+            copy(
+                out=wb_bf[e, b][:].rearrange("p (c i) j -> p c j i", i=LINE),
+                in_=wb_raw[e][:, :, b * M : (b + 1) * M].rearrange("p j (c i) -> p c j i", i=LINE),
+            )
+
+        def quantize_block(e, b, at):
+            if e not in wb_codes:
+                wb_codes[e] = made(f"wb_codes{e}", [P, N], U32, at)
+            nc.vector.quantize_mx(
+                out=wb_codes[e][:, b * M : (b + 1) * M].bitcast(FP8X4),
+                scales=wb_plane[e][:, b * M : (b + 1) * M],
+                in_=wb_bf[e, b][:].rearrange("p n j -> p (n j)"),
             )
 
         def quantize_wb(e, at):
@@ -188,40 +212,44 @@ def tile_moe_elr_s_silu_kernel(
 
         sums = {}
 
-        def frozen_layer(e, first, width):
-            acc = psum_y.tile([P, N_TILES, width], F32, name="y_acc", tag=f"y{e}_{first}")
-            sums[e, first] = acc
-            for b in range(N_TILES):
+        def frozen_layer(e, blocks, first, width, pool, tag):
+            acc = pool.tile([P, len(blocks), width], F32, name="y_acc", tag=tag)
+            sums[e, blocks[0], first] = acc
+            for k, b in enumerate(blocks):
                 for s in range(0, width, M):
                     slots = slice(first + s, first + s + M)
                     nc.tensor.matmul_mx(
-                        out=acc[:, b, s : s + M],
+                        out=acc[:, k, s : s + M],
                         lhsT=w_codes[:, e, 2 * b * M : 2 * (b + 1) * M].bitcast(FP4X4),
                         lhsT_scale=ws_plane[:, e, b * M : (b + 1) * M],
                         rhs=x_codes[e][:, slots].bitcast(FP8X4),
                         rhs_scale=x_plane[e][:, slots],
-                        start=(b == 0 and s == 0),
+                        start=(k == 0 and s == 0),
                         stop=False,
                     )
 
-        def second_layer(e, first, width, copy, queue=nc.sync):
-            acc = sums[e, first]
+        def second_layer(e, blocks, first, width):
+            acc = sums[e, blocks[0], first]
             slots = slice(first, first + width)
-            for b in range(N_TILES):
+            for k, b in enumerate(blocks):
                 cols = slice(b * M, (b + 1) * M)
                 nc.tensor.matmul_mx(
-                    out=acc[:, b, :],
+                    out=acc[:, k, :],
                     lhsT=wb_codes[e][:, cols].bitcast(FP8X4),
                     lhsT_scale=wb_plane[e][:, cols],
                     rhs=h_codes[e][:, slots].bitcast(FP8X4),
                     rhs_scale=h_plane[e][:, slots],
                     start=False,
-                    stop=(b == N_TILES - 1),
+                    stop=(k == len(blocks) - 1),
                 )
-            y = keep.tile([P, N_TILES, width], F32, name=f"y{e}_{first}")
-            copy(out=y[:], in_=acc[:])
-            columns = out[:, e * C + first : e * C + first + width]
-            queue.dma_start(out=columns.rearrange("(b p) j -> p b j", p=P), in_=y[:])
+
+        def leave(e, blocks, first, width, copy, part=None, queue=nc.sync):
+            acc = sums[e, blocks[0], first]
+            ks = range(len(blocks)) if part is None else range(part, part + 1)
+            y = keep.tile([P, len(ks), width], F32, name=f"y{e}_{blocks[ks[0]]}_{first}")
+            copy(out=y[:], in_=acc[:, ks[0] : ks[-1] + 1, :])
+            rows = out[blocks[ks[0]] * M : (blocks[ks[-1]] + 1) * M, e * C + first : e * C + first + width]
+            queue.dma_start(out=rows.rearrange("(b p) j -> p b j", p=P), in_=y[:])
 
         def first_layer(e, at):
             tile = made(f"h_bf{e}", [P, C, PACK], BF16, at)
@@ -238,35 +266,43 @@ def tile_moe_elr_s_silu_kernel(
 
         gather_words(0, 2, None)
         gather_scales(0, 2, None)
-        round_wb(0, nc.scalar.copy)
         permute_words(0)
         permute_words(1)
+        round_wb(0, nc.scalar.copy)
         permute_scales(slice(0, 1))
         permute_scales(slice(1, E))
-        first_layer(0, None)
+        first_layer(0, WB_AT + 1024)
         first_layer(1, None)
+        permute_words(2)
         gather_words(2, 1, WAS_AT)
         gather_scales(2, 1, WAS_AT + 1024)
-        permute_words(2)
         first_layer_half(2, 0, None)
         first_layer_half(2, 1, None)
-        frozen_layer(0, 0, C)
+        frozen_layer(0, [0, 1], 0, C, psum_y, "y0")
         quantize_wb(0, WA_AT + 2 * 4 * H)
         hidden_codes(0, WA_AT + 2 * 4 * H + 1024)
         quantize_hidden(0, slice(0, C))
-        round_wb(1, nc.vector.tensor_copy)
-        second_layer(0, 0, C, nc.scalar.copy)
-        hidden_codes(1, WB_AT + 4 * PACK * N)
+        round_wb(1, nc.vector.tensor_copy, "wa_codes1")
+        second_layer(0, [0, 1], 0, C)
+        leave(0, [0, 1], 0, C, nc.scalar.copy, 0)
+        leave(0, [0, 1], 0, C, nc.scalar.copy, 1)
+        hidden_codes(1, WB_AT + 1024)
         quantize_hidden(1, slice(0, C))
         quantize_wb(1, None)
         round_wb(2, nc.vector.tensor_copy)
-        frozen_layer(1, 0, C)
-        second_layer(1, 0, C, nc.scalar.copy)
-        frozen_layer(2, 0, M)
-        frozen_layer(2, M, M)
-        hidden_codes(2, WB_AT + 8 * PACK * N)
+        frozen_layer(1, [0], 0, C, psum_y, "y1")
+        frozen_layer(1, [1], 0, C, psum_h, "h_acc")
+        second_layer(1, [0], 0, C)
+        second_layer(1, [1], 0, C)
+        leave(1, [0], 0, C, nc.scalar.copy)
+        frozen_layer(2, [0, 1], 0, M, psum_y, "y2")
+        frozen_layer(2, [0, 1], M, M, psum_y, "y3")
+        hidden_codes(2, None)
         quantize_hidden(2, slice(0, M))
         quantize_wb(2, None)
         quantize_hidden(2, slice(M, C))
-        second_layer(2, 0, M, nc.scalar.copy)
-        second_layer(2, M, M, nc.vector.tensor_copy)
+        leave(1, [1], 0, C, nc.vector.tensor_copy)
+        second_layer(2, [0, 1], 0, M)
+        leave(2, [0, 1], 0, M, nc.scalar.copy)
+        second_layer(2, [0, 1], M, M)
+        leave(2, [0, 1], M, M, nc.vector.tensor_copy)

@@ -81,8 +81,7 @@ def tile_moe_elr_s_silu_kernel(
         nc.vector.memset(was_raw[:].rearrange("p e i -> p (e i)").bitcast(I32), 0)
         warm_in = keep.tile([P, 1], F32, name="warm_in")
         warm_out = keep.tile([P, 1], F32, name="warm_out")
-        nc.gpsimd.memset(warm_in[:], 0.0)
-        nc.scalar.activation(warm_out[:], warm_in[:], SILU)
+        nc.vector.memset(warm_in[:], 0.0)
         nc.gpsimd.memset(ws_plane[:].rearrange("p e n -> p (e n)").bitcast(I32), 0)
 
         def load_wa(e):
@@ -101,27 +100,37 @@ def tile_moe_elr_s_silu_kernel(
         def load_was(queue):
             load_scale_rows(queue, was_raw[:].bitcast(I32), wa_scales[:, 0].rearrange("e b i -> b e i").bitcast(I32))
 
-        def load_ws(queue):
-            load_scale_rows(queue, ws_plane[:].bitcast(I32), w_scales[:, 0].rearrange("e b n -> b e n").bitcast(I32))
+        def load_ws(r):
+            rows = w_scales[:, 0].rearrange("e b n -> b e n").bitcast(I32)
+            nc.sync.dma_start(out=ws_plane[:].bitcast(I32)[r:P:32], in_=rows[r:16:4])
 
         def load_x():
             nc.sync.dma_start(out=x_window[:].bitcast(I32), in_=x_words[0].rearrange("p t d -> p (t d)").bitcast(I32))
 
-        def load_xs(queue):
-            load_scale_rows(queue, xs_window[:].bitcast(I32), x_scales[0].bitcast(I32))
+        def load_xs(queue, r):
+            queue.dma_start(out=xs_window[:].bitcast(I32)[r:P:32], in_=x_scales[0].bitcast(I32)[r:16:4])
+
+        def warm_up():
+            nc.scalar.activation(warm_out[:], warm_in[:], SILU)
 
         nc.sync.dma_start(offsets[:], offs)
+        load_xs(nc.sync, 0)
+        load_xs(nc.sync, 1)
+        load_xs(nc.scalar, 2)
+        load_xs(nc.scalar, 3)
+        warm_up()
+        load_was(nc.scalar)
         load_x()
-        load_xs(nc.sync)
         load_wa(0)
-        load_wa(1)
         load_wb(0)
-        load_was(nc.sync)
+        load_ws(0)
+        load_wa(1)
         load_wa(2)
         load_wb(1)
         load_wb(2)
         load_w()
-        load_ws(nc.sync)
+        for r in range(1, 4):
+            load_ws(r)
 
         def gather(into, window, dtype, name, first, count, at):
             tile = made(f"{name}{first}", [P, count * C], dtype, at)
@@ -243,10 +252,10 @@ def tile_moe_elr_s_silu_kernel(
                     stop=(k == len(blocks) - 1),
                 )
 
-        def leave(e, blocks, first, width, copy, part=None, queue=nc.sync):
+        def leave(e, blocks, first, width, copy, part=None, queue=nc.sync, at=None):
             acc = sums[e, blocks[0], first]
             ks = range(len(blocks)) if part is None else range(part, part + 1)
-            y = keep.tile([P, len(ks), width], F32, name=f"y{e}_{blocks[ks[0]]}_{first}")
+            y = made(f"y{e}_{blocks[ks[0]]}_{first}", [P, len(ks), width], F32, at)
             copy(out=y[:], in_=acc[:, ks[0] : ks[-1] + 1, :])
             rows = out[blocks[ks[0]] * M : (blocks[ks[-1]] + 1) * M, e * C + first : e * C + first + width]
             queue.dma_start(out=rows.rearrange("(b p) j -> p b j", p=P), in_=y[:])
@@ -264,39 +273,39 @@ def tile_moe_elr_s_silu_kernel(
             h_bf[e, s] = tile[:]
             hidden(e, s)
 
-        gather_words(0, 2, None)
         gather_scales(0, 2, None)
-        permute_words(0)
-        permute_words(1)
+        gather_words(0, 2, None)
         round_wb(0, nc.scalar.copy)
+        permute_words(0)
         permute_scales(slice(0, 1))
         permute_scales(slice(1, E))
+        permute_words(1)
         first_layer(0, WB_AT + 1024)
         first_layer(1, None)
-        permute_words(2)
         gather_words(2, 1, WAS_AT)
         gather_scales(2, 1, WAS_AT + 1024)
+        quantize_wb(0, WAS_AT + 1280)
+        permute_words(2)
         first_layer_half(2, 0, None)
         first_layer_half(2, 1, None)
         frozen_layer(0, [0, 1], 0, C, psum_y, "y0")
-        quantize_wb(0, WA_AT + 2 * 4 * H)
-        hidden_codes(0, WA_AT + 2 * 4 * H + 1024)
+        hidden_codes(0, None)
         quantize_hidden(0, slice(0, C))
         round_wb(1, nc.vector.tensor_copy, "wa_codes1")
         second_layer(0, [0, 1], 0, C)
+        frozen_layer(2, [0, 1], 0, M, psum_y, "y2")
+        frozen_layer(2, [0, 1], M, M, psum_y, "y3")
+        frozen_layer(1, [0], 0, C, psum_y, "y1")
+        frozen_layer(1, [1], 0, C, psum_h, "h_acc")
         leave(0, [0, 1], 0, C, nc.scalar.copy, 0)
         leave(0, [0, 1], 0, C, nc.scalar.copy, 1)
         hidden_codes(1, WB_AT + 1024)
         quantize_hidden(1, slice(0, C))
         quantize_wb(1, None)
         round_wb(2, nc.vector.tensor_copy)
-        frozen_layer(1, [0], 0, C, psum_y, "y1")
-        frozen_layer(1, [1], 0, C, psum_h, "h_acc")
         second_layer(1, [0], 0, C)
         second_layer(1, [1], 0, C)
         leave(1, [0], 0, C, nc.scalar.copy)
-        frozen_layer(2, [0, 1], 0, M, psum_y, "y2")
-        frozen_layer(2, [0, 1], M, M, psum_y, "y3")
         hidden_codes(2, None)
         quantize_hidden(2, slice(0, M))
         quantize_wb(2, None)

@@ -147,10 +147,10 @@ def tile_moe_elr_s_silu_kernel(
         def hidden_codes(e, at):
             h_codes[e] = made(f"h_codes{e}", [P, C], U32, at)
 
-        def permute_words(e):
-            nc.vector.tensor_copy(
-                out=wa_codes[e][:].rearrange("p (t c i) -> p c t i", t=PACK, i=LINE),
-                in_=wa_raw[e][:].rearrange("p (c i t) -> p c t i", t=PACK, i=LINE),
+        def permute_words(e, copy=nc.vector.tensor_copy):
+            copy(
+                out=wa_codes[e][:].bitcast(U32).rearrange("p (t c i) -> p c t i", t=PACK, i=LINE),
+                in_=wa_raw[e][:].bitcast(U32).rearrange("p (c i t) -> p c t i", t=PACK, i=LINE),
             )
 
         def permute_scales(experts):
@@ -275,8 +275,8 @@ def tile_moe_elr_s_silu_kernel(
 
         gather_scales(0, 2, None)
         gather_words(0, 2, None)
+        permute_words(0, nc.scalar.copy)
         round_wb(0, nc.scalar.copy)
-        permute_words(0)
         permute_scales(slice(0, 1))
         permute_scales(slice(1, E))
         permute_words(1)
@@ -285,7 +285,7 @@ def tile_moe_elr_s_silu_kernel(
         gather_words(2, 1, WAS_AT)
         gather_scales(2, 1, WAS_AT + 1024)
         quantize_wb(0, WAS_AT + 1280)
-        permute_words(2)
+        permute_words(2, nc.scalar.copy)
         first_layer_half(2, 0, None)
         first_layer_half(2, 1, None)
         frozen_layer(0, [0, 1], 0, C, psum_y, "y0")

@@ -285,7 +285,7 @@ def tile_moe_elr_s_silu_kernel(
         gather_words(2, 1, WAS_AT)
         gather_scales(2, 1, WAS_AT + 1024)
         quantize_wb(0, WAS_AT + 1280)
-        permute_words(2, nc.scalar.copy)
+        permute_words(2)
         first_layer_half(2, 0, None)
         first_layer_half(2, 1, None)
         frozen_layer(0, [0, 1], 0, C, psum_y, "y0")

@@ -13,24 +13,18 @@ U16 = mybir.dt.uint16
 U8 = mybir.dt.uint8
 FP8X4 = mybir.dt.float8_e4m3fn_x4
 FP4X4 = mybir.dt.float4_e2m1fn_x4
-ALU = mybir.AluOpType
 SILU = mybir.ActivationFunctionType.Silu
 
 P = 128
 PACK = 4
 LINE = 4
 M = 128
-HALVES = C // M
-N_TILES = N // M
 COLS = C // 16
 WAS_AT = 0
-WA_AT = 2048
+WA_AT = 2560
 WB_AT = WA_AT + E * 4 * H
-
-
-def load_scale_rows(queue, plane, rows):
-    for r in range(4):
-        queue.dma_start(out=plane[r:P:32], in_=rows[r:16:4])
+WA_BYTES = 4 * H
+WB_BYTES = 4 * PACK * N
 
 
 def tile_moe_elr_s_silu_kernel(
@@ -44,93 +38,67 @@ def tile_moe_elr_s_silu_kernel(
         psum_h = ctx.enter_context(tc.psum_pool(name="psum_h", bufs=4))
         psum_y = ctx.enter_context(tc.psum_pool(name="psum_y", bufs=1))
 
-        def per_expert(name, shape, dtype):
-            return [keep.tile(shape, dtype, name=f"{name}{e}", tag=f"{name}{e}", align_bytes=64) for e in range(E)]
+        def made(name, shape, dtype, at=None):
+            if at is None:
+                return keep.tile(shape, dtype, name=name, align_bytes=64)
+            if isinstance(at, str):
+                return keep.tile(shape, dtype, name=name, tag=at, align_bytes=64)
+            return shared.tile(shape, dtype, name=name, align_bytes=64, offset=at)
 
         offsets = lists.tile([P, T // 16], U16, name="offsets")
-        x_window = keep.tile([P, T], U32, name="x_window", align_bytes=64)
-        xs_window = keep.tile([P, T], U8, name="xs_window", align_bytes=64)
-        def placed(name, shape, dtype, offset):
-            return shared.tile(shape, dtype, name=name, align_bytes=64, offset=offset)
-
-        was_raw = placed("was_raw", [P, E, H], U8, WAS_AT)
-        wa_raw = [placed(f"wa_raw{e}", [P, H], I32, WA_AT + e * 4 * H) for e in range(E)]
-        wb_raw = [placed(f"wb_raw{e}", [P, PACK, N], F32, WB_AT + e * 4 * PACK * N) for e in range(E)]
-        ws_plane = keep.tile([P, E, N], U8, name="ws_plane", align_bytes=64)
-        w_codes = keep.tile([P, E, 2 * N], U8, name="w_codes", align_bytes=64)
-        wa_codes = per_expert("wa_codes", [P, H], I32)
-        wa_plane = keep.tile([P, E, H], U8, name="wa_plane", align_bytes=64)
+        x_window = made("x_window", [P, T], U32)
+        xs_window = made("xs_window", [P, T], U8)
+        was_raw = made("was_raw", [P, E, H], U8, WAS_AT)
+        wa_raw = [made(f"wa_raw{e}", [P, H], U32, WA_AT + e * WA_BYTES) for e in range(E)]
+        wb_raw = [made(f"wb_raw{e}", [P, PACK, N], F32, WB_AT + e * WB_BYTES) for e in range(E)]
+        ws_plane = made("ws_plane", [P, E, N], U8)
+        w_codes = made("w_codes", [P, E, 2 * N], U8)
+        wa_plane = made("wa_plane", [P, E, H], U8)
+        wb_plane = [made(f"wb_plane{e}", [P, N], U8) for e in range(E)]
+        h_plane = [made(f"h_plane{e}", [P, C], U8) for e in range(E)]
+        wa_codes = {}
         wb_bf = {}
-        wb_plane = per_expert("wb_plane", [P, N], U8)
-        h_plane = per_expert("h_plane", [P, C], U8)
         wb_codes = {}
         x_codes = {}
         x_plane = {}
         h_codes = {}
         h_bf = {}
-        h_in = {}
+        sums = {}
 
-        def made(name, shape, dtype, at):
-            if at is None:
-                return keep.tile(shape, dtype, name=name, align_bytes=64)
-            if isinstance(at, str):
-                return keep.tile(shape, dtype, name=name, tag=at, align_bytes=64)
-            return placed(name, shape, dtype, at)
-
-        nc.vector.memset(xs_window[:].bitcast(I32), 0)
-        nc.vector.memset(was_raw[:].rearrange("p e i -> p (e i)").bitcast(I32), 0)
         warm_in = keep.tile([P, 1], F32, name="warm_in")
         warm_out = keep.tile([P, 1], F32, name="warm_out")
+        nc.vector.memset(xs_window[:].bitcast(I32), 0)
+        nc.vector.memset(was_raw[:].rearrange("p e i -> p (e i)").bitcast(I32), 0)
         nc.vector.memset(warm_in[:], 0.0)
         nc.gpsimd.memset(ws_plane[:].rearrange("p e n -> p (e n)").bitcast(I32), 0)
-
-        def load_wa(e):
-            nc.sync.dma_start(out=wa_raw[e][:], in_=wa_words[e, 0].rearrange("p i d -> p (i d)").bitcast(I32))
-
-        def load_wb(e):
-            nc.sync.dma_start(out=wb_raw[e][:], in_=wb[e].rearrange("(p j) n -> p j n", j=PACK))
-
-        def load_wb_rows(e, first):
-            rows = wb[e].rearrange("(p j) n -> p j n", j=PACK)
-            nc.sync.dma_start(out=wb_raw[e][:, first : first + 2, :], in_=rows[:, first : first + 2, :])
-
-        def load_w():
-            nc.sync.dma_start(out=w_codes[:].bitcast(I32), in_=w_words[:, 0].rearrange("e p b -> p e b").bitcast(I32))
-
-        def load_was(queue):
-            load_scale_rows(queue, was_raw[:].bitcast(I32), wa_scales[:, 0].rearrange("e b i -> b e i").bitcast(I32))
-
-        def load_ws(r):
-            rows = w_scales[:, 0].rearrange("e b n -> b e n").bitcast(I32)
-            nc.sync.dma_start(out=ws_plane[:].bitcast(I32)[r:P:32], in_=rows[r:16:4])
 
         def load_x():
             nc.sync.dma_start(out=x_window[:].bitcast(I32), in_=x_words[0].rearrange("p t d -> p (t d)").bitcast(I32))
 
+        def load_wa(e):
+            words = wa_words[e, 0].rearrange("p i d -> p (i d)").bitcast(I32)
+            nc.sync.dma_start(out=wa_raw[e][:].bitcast(I32), in_=words)
+
+        def load_wb(e):
+            nc.sync.dma_start(out=wb_raw[e][:], in_=wb[e].rearrange("(p j) n -> p j n", j=PACK))
+
+        def load_w(first, count):
+            words = w_words[first : first + count, 0].rearrange("e p b -> p e b").bitcast(I32)
+            nc.sync.dma_start(out=w_codes[:, first : first + count, :].bitcast(I32), in_=words)
+
         def load_xs(queue, r):
             queue.dma_start(out=xs_window[:].bitcast(I32)[r:P:32], in_=x_scales[0].bitcast(I32)[r:16:4])
 
+        def load_was(queue, r):
+            rows = wa_scales[:, 0].rearrange("e b i -> b e i").bitcast(I32)
+            queue.dma_start(out=was_raw[:].bitcast(I32)[r:P:32], in_=rows[r:16:4])
+
+        def load_ws(queue, r):
+            rows = w_scales[:, 0].rearrange("e b n -> b e n").bitcast(I32)
+            queue.dma_start(out=ws_plane[:].bitcast(I32)[r:P:32], in_=rows[r:16:4])
+
         def warm_up():
             nc.scalar.activation(warm_out[:], warm_in[:], SILU)
-
-        nc.sync.dma_start(offsets[:], offs)
-        load_xs(nc.sync, 0)
-        load_xs(nc.sync, 1)
-        load_xs(nc.scalar, 2)
-        load_xs(nc.scalar, 3)
-        warm_up()
-        load_was(nc.scalar)
-        load_x()
-        load_wa(0)
-        load_wb(0)
-        load_ws(0)
-        load_wa(1)
-        load_wa(2)
-        load_wb(1)
-        load_wb(2)
-        load_w()
-        for r in range(1, 4):
-            load_ws(r)
 
         def gather(into, window, dtype, name, first, count, at):
             tile = made(f"{name}{first}", [P, count * C], dtype, at)
@@ -138,65 +106,45 @@ def tile_moe_elr_s_silu_kernel(
             for e in range(count):
                 into[first + e] = tile[:, e * C : (e + 1) * C]
 
-        def gather_words(first, count, at):
+        def gather_words(first, count, at=None):
             gather(x_codes, x_window, U32, "x_codes", first, count, at)
 
-        def gather_scales(first, count, at):
+        def gather_scales(first, count, at=None):
             gather(x_plane, xs_window, U8, "x_plane", first, count, at)
 
-        def hidden_codes(e, at):
-            h_codes[e] = made(f"h_codes{e}", [P, C], U32, at)
-
-        def permute_words(e, copy=nc.vector.tensor_copy):
+        def reorder_words(e, copy, at=None):
+            wa_codes[e] = made(f"wa_codes{e}", [P, H], U32, at)
             copy(
-                out=wa_codes[e][:].bitcast(U32).rearrange("p (t c i) -> p c t i", t=PACK, i=LINE),
-                in_=wa_raw[e][:].bitcast(U32).rearrange("p (c i t) -> p c t i", t=PACK, i=LINE),
+                out=wa_codes[e][:].rearrange("p (t c i) -> p c t i", t=PACK, i=LINE),
+                in_=wa_raw[e][:].rearrange("p (c i t) -> p c t i", t=PACK, i=LINE),
             )
 
-        def permute_scales(experts):
+        def reorder_scales(first, count):
+            experts = slice(first, first + count)
             nc.vector.tensor_copy(
                 out=wa_plane[:, experts, :].rearrange("p e (t h m) -> p h e t m", t=PACK, h=2),
                 in_=was_raw[:, experts, :].rearrange("p e (h m t) -> p h e t m", t=PACK, h=2),
             )
 
-        def round_wb(e, copy, at=None):
-            wb_bf[e] = made(f"wb_bf{e}", [P, N, PACK], BF16, at)
+        def round_wb(e, first, width, copy, at=None):
+            wb_bf[e, first] = made(f"wb_bf{e}_{first}", [P, width, PACK], BF16, at)
             copy(
-                out=wb_bf[e][:].rearrange("p (c i) j -> p c j i", i=LINE),
-                in_=wb_raw[e][:].rearrange("p j (c i) -> p c j i", i=LINE),
+                out=wb_bf[e, first][:].rearrange("p (c i) j -> p c j i", i=LINE),
+                in_=wb_raw[e][:, :, first : first + width].rearrange("p j (c i) -> p c j i", i=LINE),
             )
 
-        def round_wb_pool(e, at):
-            wb_bf[e] = made(f"wb_bf{e}", [P, N, PACK], BF16, at)
-            nc.gpsimd.tensor_scalar(
-                wb_bf[e][:], wb_raw[e][:].rearrange("p j n -> p n j"), 1.0, 0.0, op0=ALU.mult, op1=ALU.add
-            )
-
-        def round_block(e, b, copy, at=None):
-            wb_bf[e, b] = made(f"wb_bf{e}_{b}", [P, M, PACK], BF16, at)
-            copy(
-                out=wb_bf[e, b][:].rearrange("p (c i) j -> p c j i", i=LINE),
-                in_=wb_raw[e][:, :, b * M : (b + 1) * M].rearrange("p j (c i) -> p c j i", i=LINE),
-            )
-
-        def quantize_block(e, b, at):
+        def quantize_wb(e, first, width, at=None):
             if e not in wb_codes:
                 wb_codes[e] = made(f"wb_codes{e}", [P, N], U32, at)
             nc.vector.quantize_mx(
-                out=wb_codes[e][:, b * M : (b + 1) * M].bitcast(FP8X4),
-                scales=wb_plane[e][:, b * M : (b + 1) * M],
-                in_=wb_bf[e, b][:].rearrange("p n j -> p (n j)"),
+                out=wb_codes[e][:, first : first + width].bitcast(FP8X4),
+                scales=wb_plane[e][:, first : first + width],
+                in_=wb_bf[e, first][:].rearrange("p n j -> p (n j)"),
             )
 
-        def quantize_wb(e, at):
-            wb_codes[e] = made(f"wb_codes{e}", [P, N], U32, at)
-            nc.vector.quantize_mx(
-                out=wb_codes[e][:].bitcast(FP8X4),
-                scales=wb_plane[e][:],
-                in_=wb_bf[e][:].rearrange("p n j -> p (n j)"),
-            )
-
-        def hidden(e, s):
+        def first_layer(e, s, at=None):
+            if e not in h_bf:
+                h_bf[e] = made(f"h_bf{e}", [P, C, PACK], BF16, at)
             slots = slice(s * M, (s + 1) * M)
             acc = psum_h.tile([P, PACK, M], F32, name="h_acc")
             for t in range(PACK):
@@ -210,34 +158,35 @@ def tile_moe_elr_s_silu_kernel(
                     start=True,
                     stop=True,
                 )
-            nc.scalar.activation(h_bf[e, s], acc[:].rearrange("p t u -> p u t"), SILU)
+            nc.scalar.activation(h_bf[e][:, slots, :], acc[:].rearrange("p t u -> p u t"), SILU)
 
-        def quantize_hidden(e, slots):
+        def quantize_hidden(e, first, width, at=None):
+            h_codes[e, first] = made(f"h_codes{e}_{first}", [P, width], U32, at)
+            slots = slice(first, first + width)
             nc.vector.quantize_mx(
-                out=h_codes[e][:, slots].bitcast(FP8X4),
+                out=h_codes[e, first][:].bitcast(FP8X4),
                 scales=h_plane[e][:, slots],
-                in_=h_in[e, slots.start].rearrange("p u t -> p (u t)"),
+                in_=h_bf[e][:, slots, :].rearrange("p u t -> p (u t)"),
             )
 
-        sums = {}
+        def bank(e, blocks, first, width, pool, tag):
+            sums[e, blocks[0], first] = pool.tile([P, len(blocks), width], F32, name="y_acc", tag=tag)
 
-        def frozen_layer(e, blocks, first, width, pool, tag):
-            acc = pool.tile([P, len(blocks), width], F32, name="y_acc", tag=tag)
-            sums[e, blocks[0], first] = acc
+        def frozen_layer(e, blocks, first, width, opens):
+            acc = sums[e, blocks[0], first]
+            slots = slice(first, first + width)
             for k, b in enumerate(blocks):
-                for s in range(0, width, M):
-                    slots = slice(first + s, first + s + M)
-                    nc.tensor.matmul_mx(
-                        out=acc[:, k, s : s + M],
-                        lhsT=w_codes[:, e, 2 * b * M : 2 * (b + 1) * M].bitcast(FP4X4),
-                        lhsT_scale=ws_plane[:, e, b * M : (b + 1) * M],
-                        rhs=x_codes[e][:, slots].bitcast(FP8X4),
-                        rhs_scale=x_plane[e][:, slots],
-                        start=(k == 0 and s == 0),
-                        stop=False,
-                    )
+                nc.tensor.matmul_mx(
+                    out=acc[:, k, :],
+                    lhsT=w_codes[:, e, 2 * b * M : 2 * (b + 1) * M].bitcast(FP4X4),
+                    lhsT_scale=ws_plane[:, e, b * M : (b + 1) * M],
+                    rhs=x_codes[e][:, slots].bitcast(FP8X4),
+                    rhs_scale=x_plane[e][:, slots],
+                    start=(opens and k == 0),
+                    stop=(not opens and k == len(blocks) - 1),
+                )
 
-        def second_layer(e, blocks, first, width):
+        def second_layer(e, blocks, first, width, opens):
             acc = sums[e, blocks[0], first]
             slots = slice(first, first + width)
             for k, b in enumerate(blocks):
@@ -246,72 +195,86 @@ def tile_moe_elr_s_silu_kernel(
                     out=acc[:, k, :],
                     lhsT=wb_codes[e][:, cols].bitcast(FP8X4),
                     lhsT_scale=wb_plane[e][:, cols],
-                    rhs=h_codes[e][:, slots].bitcast(FP8X4),
+                    rhs=h_codes[e, first][:].bitcast(FP8X4),
                     rhs_scale=h_plane[e][:, slots],
-                    start=False,
-                    stop=(k == len(blocks) - 1),
+                    start=(opens and k == 0),
+                    stop=(not opens and k == len(blocks) - 1),
                 )
 
-        def leave(e, blocks, first, width, copy, part=None, queue=nc.sync, at=None):
+        def leave(e, blocks, first, width, copy, part=None, at=None):
             acc = sums[e, blocks[0], first]
             ks = range(len(blocks)) if part is None else range(part, part + 1)
             y = made(f"y{e}_{blocks[ks[0]]}_{first}", [P, len(ks), width], F32, at)
             copy(out=y[:], in_=acc[:, ks[0] : ks[-1] + 1, :])
             rows = out[blocks[ks[0]] * M : (blocks[ks[-1]] + 1) * M, e * C + first : e * C + first + width]
-            queue.dma_start(out=rows.rearrange("(b p) j -> p b j", p=P), in_=y[:])
+            nc.sync.dma_start(out=rows.rearrange("(b p) j -> p b j", p=P), in_=y[:])
 
-        def first_layer(e, at):
-            tile = made(f"h_bf{e}", [P, C, PACK], BF16, at)
-            h_in[e, 0] = tile[:]
-            for s in range(HALVES):
-                h_bf[e, s] = tile[:, s * M : (s + 1) * M, :]
-                hidden(e, s)
+        on_vector = nc.vector.tensor_copy
+        on_scalar = nc.scalar.copy
 
-        def first_layer_half(e, s, at):
-            tile = made(f"h_bf{e}_{s}", [P, M, PACK], BF16, at)
-            h_in[e, s * M] = tile[:]
-            h_bf[e, s] = tile[:]
-            hidden(e, s)
+        nc.sync.dma_start(offsets[:], offs)
+        load_x()
+        load_xs(nc.sync, 2)
+        load_xs(nc.scalar, 0)
+        load_xs(nc.scalar, 1)
+        warm_up()
+        for r in range(4):
+            load_was(nc.scalar, r)
+        load_wa(0)
+        load_xs(nc.sync, 3)
+        load_wb(0)
+        load_ws(nc.sync, 0)
+        load_wa(1)
+        load_wa(2)
+        load_wb(1)
+        load_wb(2)
+        load_w(0, E)
+        for r in range(1, 4):
+            load_ws(nc.sync, r)
 
-        gather_scales(0, 2, None)
-        gather_words(0, 2, None)
-        permute_words(0, nc.scalar.copy)
-        round_wb(0, nc.scalar.copy)
-        permute_scales(slice(0, 1))
-        permute_scales(slice(1, E))
-        permute_words(1)
-        first_layer(0, WB_AT + 1024)
-        first_layer(1, None)
+        gather_words(0, 2)
+        gather_scales(0, 2)
+        reorder_words(0, on_scalar)
+        round_wb(0, 0, N, on_scalar, "wb_bf0")
+        reorder_scales(0, 1)
+        reorder_scales(1, 2)
+        reorder_words(1, on_vector, "wa_codes1")
+        first_layer(0, 0, WB_AT + 1024)
+        first_layer(0, 1)
+        first_layer(1, 0)
+        first_layer(1, 1)
         gather_words(2, 1, WAS_AT)
         gather_scales(2, 1, WAS_AT + 1024)
-        quantize_wb(0, WAS_AT + 1280)
-        permute_words(2)
-        first_layer_half(2, 0, None)
-        first_layer_half(2, 1, None)
-        frozen_layer(0, [0, 1], 0, C, psum_y, "y0")
-        hidden_codes(0, None)
-        quantize_hidden(0, slice(0, C))
-        round_wb(1, nc.vector.tensor_copy, "wa_codes1")
-        second_layer(0, [0, 1], 0, C)
-        frozen_layer(2, [0, 1], 0, M, psum_y, "y2")
-        frozen_layer(2, [0, 1], M, M, psum_y, "y3")
-        frozen_layer(1, [0], 0, C, psum_y, "y1")
-        frozen_layer(1, [1], 0, C, psum_h, "h_acc")
-        leave(0, [0, 1], 0, C, nc.scalar.copy, 0)
-        leave(0, [0, 1], 0, C, nc.scalar.copy, 1)
-        hidden_codes(1, WB_AT + 1024)
-        quantize_hidden(1, slice(0, C))
-        quantize_wb(1, None)
-        round_wb(2, nc.vector.tensor_copy)
-        second_layer(1, [0], 0, C)
-        second_layer(1, [1], 0, C)
-        leave(1, [0], 0, C, nc.scalar.copy)
-        hidden_codes(2, None)
-        quantize_hidden(2, slice(0, M))
-        quantize_wb(2, None)
-        quantize_hidden(2, slice(M, C))
-        leave(1, [1], 0, C, nc.vector.tensor_copy)
-        second_layer(2, [0, 1], 0, M)
-        leave(2, [0, 1], 0, M, nc.scalar.copy)
-        second_layer(2, [0, 1], M, M)
-        leave(2, [0, 1], M, M, nc.vector.tensor_copy)
+        reorder_words(2, on_vector)
+        quantize_wb(0, 0, N, WAS_AT + 1280)
+        first_layer(2, 0)
+        first_layer(2, 1)
+        round_wb(1, 0, N, on_vector, "wa_codes1")
+        quantize_hidden(0, 0, C, "wb_bf0")
+        quantize_wb(1, 0, N)
+        round_wb(2, 0, N, on_vector)
+        quantize_hidden(1, 0, C, WB_AT + 1024)
+        quantize_hidden(2, 0, M, "wa_codes1")
+        quantize_wb(2, 0, N)
+        quantize_hidden(2, M, M)
+        bank(0, [0, 1], 0, C, psum_y, "y0")
+        bank(1, [0], 0, C, psum_y, "y1")
+        bank(1, [1], 0, C, psum_h, "h_acc")
+        bank(2, [0, 1], 0, M, psum_y, "y2")
+        bank(2, [0, 1], M, M, psum_y, "y3")
+        second_layer(0, [0, 1], 0, C, True)
+        frozen_layer(0, [0, 1], 0, C, False)
+        frozen_layer(1, [0], 0, C, True)
+        frozen_layer(1, [1], 0, C, True)
+        second_layer(1, [0], 0, C, False)
+        second_layer(1, [1], 0, C, False)
+        frozen_layer(2, [0, 1], 0, M, True)
+        frozen_layer(2, [0, 1], M, M, True)
+        second_layer(2, [0, 1], 0, M, False)
+        second_layer(2, [0, 1], M, M, False)
+        leave(0, [0, 1], 0, C, on_scalar, 0)
+        leave(0, [0, 1], 0, C, on_scalar, 1)
+        leave(1, [0], 0, C, on_scalar)
+        leave(1, [1], 0, C, on_vector)
+        leave(2, [0, 1], 0, M, on_scalar)
+        leave(2, [0, 1], M, M, on_vector)

@@ -266,10 +266,10 @@ def tile_moe_elr_s_silu_kernel(
         frozen_layer(0, [0, 1], 0, C, False)
         frozen_layer(1, [0], 0, C, True)
         frozen_layer(1, [1], 0, C, True)
-        second_layer(1, [0], 0, C, False)
-        second_layer(1, [1], 0, C, False)
         frozen_layer(2, [0, 1], 0, M, True)
         frozen_layer(2, [0, 1], M, M, True)
+        second_layer(1, [0], 0, C, False)
+        second_layer(1, [1], 0, C, False)
         second_layer(2, [0, 1], 0, M, False)
         second_layer(2, [0, 1], M, M, False)
         leave(0, [0, 1], 0, C, on_scalar, 0)

@@ -112,11 +112,12 @@ def tile_moe_elr_s_silu_kernel(
         def gather_scales(first, count, at=None):
             gather(x_plane, xs_window, U8, "x_plane", first, count, at)
 
-        def reorder_words(e, copy, at=None):
-            wa_codes[e] = made(f"wa_codes{e}", [P, H], U32, at)
+        def reorder_words(e, copy, at=None, lines=slice(0, M // LINE)):
+            if e not in wa_codes:
+                wa_codes[e] = made(f"wa_codes{e}", [P, H], U32, at)
             copy(
-                out=wa_codes[e][:].rearrange("p (t c i) -> p c t i", t=PACK, i=LINE),
-                in_=wa_raw[e][:].rearrange("p (c i t) -> p c t i", t=PACK, i=LINE),
+                out=wa_codes[e][:].rearrange("p (t c i) -> p c t i", t=PACK, i=LINE)[:, lines],
+                in_=wa_raw[e][:].rearrange("p (c i t) -> p c t i", t=PACK, i=LINE)[:, lines],
             )
 
         def reorder_scales(first, count):
@@ -186,20 +187,21 @@ def tile_moe_elr_s_silu_kernel(
                     stop=(not opens and k == len(blocks) - 1),
                 )
 
-        def second_layer(e, blocks, first, width, opens):
+        def second_layer(e, blocks, first, width, opens, piece=None):
             acc = sums[e, blocks[0], first]
-            slots = slice(first, first + width)
+            piece = piece or width
             for k, b in enumerate(blocks):
                 cols = slice(b * M, (b + 1) * M)
-                nc.tensor.matmul_mx(
-                    out=acc[:, k, :],
-                    lhsT=wb_codes[e][:, cols].bitcast(FP8X4),
-                    lhsT_scale=wb_plane[e][:, cols],
-                    rhs=h_codes[e, first][:].bitcast(FP8X4),
-                    rhs_scale=h_plane[e][:, slots],
-                    start=(opens and k == 0),
-                    stop=(not opens and k == len(blocks) - 1),
-                )
+                for s in range(0, width, piece):
+                    nc.tensor.matmul_mx(
+                        out=acc[:, k, s : s + piece],
+                        lhsT=wb_codes[e][:, cols].bitcast(FP8X4),
+                        lhsT_scale=wb_plane[e][:, cols],
+                        rhs=h_codes[e, first + s][:].bitcast(FP8X4),
+                        rhs_scale=h_plane[e][:, first + s : first + s + piece],
+                        start=(opens and k == 0 and s == 0),
+                        stop=(not opens and k == len(blocks) - 1 and s + piece == width),
+                    )
 
         def leave(e, blocks, first, width, copy, part=None, at=None):
             acc = sums[e, blocks[0], first]
@@ -214,23 +216,24 @@ def tile_moe_elr_s_silu_kernel(
 
         nc.sync.dma_start(offsets[:], offs)
         load_x()
-        load_xs(nc.sync, 2)
-        load_xs(nc.scalar, 0)
-        load_xs(nc.scalar, 1)
-        warm_up()
-        for r in range(4):
-            load_was(nc.scalar, r)
-        load_wa(0)
         load_xs(nc.sync, 3)
+        for r in range(3):
+            load_xs(nc.scalar, r)
+        load_was(nc.scalar, 0)
+        warm_up()
+        load_was(nc.scalar, 1)
+        load_was(nc.scalar, 2)
+        load_wa(0)
         load_wb(0)
+        load_was(nc.sync, 3)
         load_ws(nc.sync, 0)
         load_wa(1)
         load_wa(2)
         load_wb(1)
-        load_wb(2)
         load_w(0, E)
         for r in range(1, 4):
             load_ws(nc.sync, r)
+        load_wb(2)
 
         gather_words(0, 2)
         gather_scales(0, 2)
@@ -238,7 +241,7 @@ def tile_moe_elr_s_silu_kernel(
         round_wb(0, 0, N, on_scalar, "wb_bf0")
         reorder_scales(0, 1)
         reorder_scales(1, 2)
-        reorder_words(1, on_vector, "wa_codes1")
+        reorder_words(1, on_vector)
         first_layer(0, 0, WB_AT + 1024)
         first_layer(0, 1)
         first_layer(1, 0)
@@ -249,32 +252,34 @@ def tile_moe_elr_s_silu_kernel(
         quantize_wb(0, 0, N, WAS_AT + 1280)
         first_layer(2, 0)
         first_layer(2, 1)
-        round_wb(1, 0, N, on_vector, "wa_codes1")
+        round_wb(1, 0, N, on_vector)
         quantize_hidden(0, 0, C, "wb_bf0")
         quantize_wb(1, 0, N)
-        round_wb(2, 0, N, on_vector)
         quantize_hidden(1, 0, C, WB_AT + 1024)
-        quantize_hidden(2, 0, M, "wa_codes1")
-        quantize_wb(2, 0, N)
-        quantize_hidden(2, M, M)
+        quantize_hidden(2, 0, M)
+        round_wb(2, 0, M, on_vector)
+        round_wb(2, M, M, on_vector)
+        quantize_wb(2, 0, M)
+        quantize_hidden(2, M, M, WB_AT + 2 * WB_BYTES)
+        quantize_wb(2, M, M)
         bank(0, [0, 1], 0, C, psum_y, "y0")
         bank(1, [0], 0, C, psum_y, "y1")
         bank(1, [1], 0, C, psum_h, "h_acc")
-        bank(2, [0, 1], 0, M, psum_y, "y2")
-        bank(2, [0, 1], M, M, psum_y, "y3")
+        bank(2, [0], 0, C, psum_y, "y2")
+        bank(2, [1], 0, C, psum_y, "y3")
         second_layer(0, [0, 1], 0, C, True)
         frozen_layer(0, [0, 1], 0, C, False)
         frozen_layer(1, [0], 0, C, True)
         frozen_layer(1, [1], 0, C, True)
-        frozen_layer(2, [0, 1], 0, M, True)
-        frozen_layer(2, [0, 1], M, M, True)
         second_layer(1, [0], 0, C, False)
         second_layer(1, [1], 0, C, False)
-        second_layer(2, [0, 1], 0, M, False)
-        second_layer(2, [0, 1], M, M, False)
+        frozen_layer(2, [0], 0, C, True)
+        frozen_layer(2, [1], 0, C, True)
+        second_layer(2, [0], 0, C, False, M)
+        second_layer(2, [1], 0, C, False, M)
         leave(0, [0, 1], 0, C, on_scalar, 0)
         leave(0, [0, 1], 0, C, on_scalar, 1)
         leave(1, [0], 0, C, on_scalar)
-        leave(1, [1], 0, C, on_vector)
-        leave(2, [0, 1], 0, M, on_scalar)
-        leave(2, [0, 1], M, M, on_vector)
+        leave(1, [1], 0, C, on_vector, None, WB_AT + 2 * WB_BYTES + 1024)
+        leave(2, [0], 0, C, on_scalar)
+        leave(2, [1], 0, C, on_vector)

@@ -211,6 +211,12 @@ def tile_moe_elr_s_silu_kernel(
             rows = out[blocks[ks[0]] * M : (blocks[ks[-1]] + 1) * M, e * C + first : e * C + first + width]
             nc.sync.dma_start(out=rows.rearrange("(b p) j -> p b j", p=P), in_=y[:])
 
+        def leave_in_halves(e, b, copies):
+            y = made(f"y{e}_{b}", [P, C], F32)
+            for s, copy in enumerate(copies):
+                copy(out=y[:, s * M : (s + 1) * M], in_=sums[e, b, s * M][:, 0, :])
+            nc.sync.dma_start(out=out[b * M : (b + 1) * M, e * C : (e + 1) * C], in_=y[:])
+
         on_vector = nc.vector.tensor_copy
         on_scalar = nc.scalar.copy
 
@@ -230,10 +236,11 @@ def tile_moe_elr_s_silu_kernel(
         load_wa(1)
         load_wa(2)
         load_wb(1)
-        load_w(0, E)
+        load_w(0, 2)
         for r in range(1, 4):
             load_ws(nc.sync, r)
         load_wb(2)
+        load_w(2, 1)
 
         gather_words(0, 2)
         gather_scales(0, 2)
@@ -265,21 +272,25 @@ def tile_moe_elr_s_silu_kernel(
         bank(0, [0, 1], 0, C, psum_y, "y0")
         bank(1, [0], 0, C, psum_y, "y1")
         bank(1, [1], 0, C, psum_h, "h_acc")
-        bank(2, [0], 0, C, psum_y, "y2")
-        bank(2, [1], 0, C, psum_y, "y3")
+        bank(2, [0], 0, M, psum_h, "h_acc")
+        bank(2, [0], M, M, psum_h, "h_acc")
+        bank(2, [1], 0, M, psum_y, "y2")
+        bank(2, [1], M, M, psum_y, "y3")
         second_layer(0, [0, 1], 0, C, True)
         frozen_layer(0, [0, 1], 0, C, False)
         frozen_layer(1, [0], 0, C, True)
         frozen_layer(1, [1], 0, C, True)
         second_layer(1, [0], 0, C, False)
         second_layer(1, [1], 0, C, False)
-        frozen_layer(2, [0], 0, C, True)
-        frozen_layer(2, [1], 0, C, True)
-        second_layer(2, [0], 0, C, False, M)
-        second_layer(2, [1], 0, C, False, M)
+        for b in range(2):
+            for s in range(0, C, M):
+                frozen_layer(2, [b], s, M, True)
+        for b in range(2):
+            for s in range(0, C, M):
+                second_layer(2, [b], s, M, False)
         leave(0, [0, 1], 0, C, on_scalar, 0)
         leave(0, [0, 1], 0, C, on_scalar, 1)
         leave(1, [0], 0, C, on_scalar)
-        leave(1, [1], 0, C, on_vector, None, WB_AT + 2 * WB_BYTES + 1024)
-        leave(2, [0], 0, C, on_scalar)
-        leave(2, [1], 0, C, on_vector)
+        leave(1, [1], 0, C, on_scalar)
+        leave_in_halves(2, 0, [on_scalar, on_vector])
+        leave_in_halves(2, 1, [on_scalar, on_vector])

@@ -120,11 +120,11 @@ def tile_moe_elr_s_silu_kernel(
                 in_=wa_raw[e][:].rearrange("p (c i t) -> p c t i", t=PACK, i=LINE)[:, lines],
             )
 
-        def reorder_scales(first, count):
+        def reorder_scales(first, count, passes=slice(0, PACK)):
             experts = slice(first, first + count)
             nc.vector.tensor_copy(
-                out=wa_plane[:, experts, :].rearrange("p e (t h m) -> p h e t m", t=PACK, h=2),
-                in_=was_raw[:, experts, :].rearrange("p e (h m t) -> p h e t m", t=PACK, h=2),
+                out=wa_plane[:, experts, :].rearrange("p e (t h m) -> p h e t m", t=PACK, h=2)[:, :, :, passes],
+                in_=was_raw[:, experts, :].rearrange("p e (h m t) -> p h e t m", t=PACK, h=2)[:, :, :, passes],
             )
 
         def round_wb(e, first, width, copy, at=None):
@@ -246,16 +246,18 @@ def tile_moe_elr_s_silu_kernel(
         gather_scales(0, 2)
         reorder_words(0, on_scalar)
         round_wb(0, 0, N, on_scalar, "wb_bf0")
-        reorder_scales(0, 1)
+        reorder_scales(0, 1, slice(0, 2))
+        reorder_scales(0, 1, slice(2, 4))
         reorder_scales(1, 2)
         reorder_words(1, on_vector)
+        reorder_words(2, on_scalar, None, slice(16, 32))
         first_layer(0, 0, WB_AT + 1024)
         first_layer(0, 1)
         first_layer(1, 0)
         first_layer(1, 1)
         gather_words(2, 1, WAS_AT)
         gather_scales(2, 1, WAS_AT + 1024)
-        reorder_words(2, on_vector)
+        reorder_words(2, on_vector, None, slice(0, 16))
         quantize_wb(0, 0, N, WAS_AT + 1280)
         first_layer(2, 0)
         first_layer(2, 1)

@@ -20,11 +20,12 @@ PACK = 4
 LINE = 4
 M = 128
 COLS = C // 16
-WAS_AT = 0
-WA_AT = 2560
-WB_AT = WA_AT + E * 4 * H
 WA_BYTES = 4 * H
 WB_BYTES = 4 * PACK * N
+WAS_AT = 0
+WA_AT = 2560
+WB_AT = WA_AT + E * WA_BYTES
+W_AT = WB_AT + E * WB_BYTES
 
 
 def tile_moe_elr_s_silu_kernel(
@@ -52,10 +53,10 @@ def tile_moe_elr_s_silu_kernel(
         wa_raw = [made(f"wa_raw{e}", [P, H], U32, WA_AT + e * WA_BYTES) for e in range(E)]
         wb_raw = [made(f"wb_raw{e}", [P, PACK, N], F32, WB_AT + e * WB_BYTES) for e in range(E)]
         ws_plane = made("ws_plane", [P, E, N], U8)
-        w_codes = made("w_codes", [P, E, 2 * N], U8)
         wa_plane = made("wa_plane", [P, E, H], U8)
         wb_plane = [made(f"wb_plane{e}", [P, N], U8) for e in range(E)]
         h_plane = [made(f"h_plane{e}", [P, C], U8) for e in range(E)]
+        w_codes = {}
         wa_codes = {}
         wb_bf = {}
         wb_codes = {}
@@ -63,6 +64,7 @@ def tile_moe_elr_s_silu_kernel(
         x_plane = {}
         h_codes = {}
         h_bf = {}
+        h_sums = {}
         sums = {}
 
         warm_in = keep.tile([P, 1], F32, name="warm_in")
@@ -72,19 +74,22 @@ def tile_moe_elr_s_silu_kernel(
         nc.vector.memset(warm_in[:], 0.0)
         nc.gpsimd.memset(ws_plane[:].rearrange("p e n -> p (e n)").bitcast(I32), 0)
 
-        def load_x():
-            nc.sync.dma_start(out=x_window[:].bitcast(I32), in_=x_words[0].rearrange("p t d -> p (t d)").bitcast(I32))
+        def load_x(queue):
+            queue.dma_start(out=x_window[:].bitcast(I32), in_=x_words[0].rearrange("p t d -> p (t d)").bitcast(I32))
 
-        def load_wa(e):
+        def load_wa(queue, e):
             words = wa_words[e, 0].rearrange("p i d -> p (i d)").bitcast(I32)
-            nc.sync.dma_start(out=wa_raw[e][:].bitcast(I32), in_=words)
+            queue.dma_start(out=wa_raw[e][:].bitcast(I32), in_=words)
 
-        def load_wb(e):
-            nc.sync.dma_start(out=wb_raw[e][:], in_=wb[e].rearrange("(p j) n -> p j n", j=PACK))
+        def load_wb(queue, e):
+            queue.dma_start(out=wb_raw[e][:], in_=wb[e].rearrange("(p j) n -> p j n", j=PACK))
 
-        def load_w(first, count):
+        def load_w(queue, first, count, at=None):
+            tile = made(f"w_codes{first}", [P, count, 2 * N], U8, at)
             words = w_words[first : first + count, 0].rearrange("e p b -> p e b").bitcast(I32)
-            nc.sync.dma_start(out=w_codes[:, first : first + count, :].bitcast(I32), in_=words)
+            queue.dma_start(out=tile[:].bitcast(I32), in_=words)
+            for e in range(count):
+                w_codes[first + e] = tile[:, e, :]
 
         def load_xs(queue, r):
             queue.dma_start(out=xs_window[:].bitcast(I32)[r:P:32], in_=x_scales[0].bitcast(I32)[r:16:4])
@@ -143,11 +148,10 @@ def tile_moe_elr_s_silu_kernel(
                 in_=wb_bf[e, first][:].rearrange("p n j -> p (n j)"),
             )
 
-        def first_layer(e, s, at=None):
-            if e not in h_bf:
-                h_bf[e] = made(f"h_bf{e}", [P, C, PACK], BF16, at)
+        def first_layer(e, s):
             slots = slice(s * M, (s + 1) * M)
             acc = psum_h.tile([P, PACK, M], F32, name="h_acc")
+            h_sums[e, s] = acc
             for t in range(PACK):
                 cols = slice(t * M, (t + 1) * M)
                 nc.tensor.matmul_mx(
@@ -159,7 +163,11 @@ def tile_moe_elr_s_silu_kernel(
                     start=True,
                     stop=True,
                 )
-            nc.scalar.activation(h_bf[e][:, slots, :], acc[:].rearrange("p t u -> p u t"), SILU)
+
+        def silu(e, s, at=None):
+            if e not in h_bf:
+                h_bf[e] = made(f"h_bf{e}", [P, C, PACK], BF16, at)
+            nc.scalar.activation(h_bf[e][:, s * M : (s + 1) * M, :], h_sums[e, s][:].rearrange("p t u -> p u t"), SILU)
 
         def quantize_hidden(e, first, width, at=None):
             h_codes[e, first] = made(f"h_codes{e}_{first}", [P, width], U32, at)
@@ -179,7 +187,7 @@ def tile_moe_elr_s_silu_kernel(
             for k, b in enumerate(blocks):
                 nc.tensor.matmul_mx(
                     out=acc[:, k, :],
-                    lhsT=w_codes[:, e, 2 * b * M : 2 * (b + 1) * M].bitcast(FP4X4),
+                    lhsT=w_codes[e][:, 2 * b * M : 2 * (b + 1) * M].bitcast(FP4X4),
                     lhsT_scale=ws_plane[:, e, b * M : (b + 1) * M],
                     rhs=x_codes[e][:, slots].bitcast(FP8X4),
                     rhs_scale=x_plane[e][:, slots],
@@ -187,29 +195,27 @@ def tile_moe_elr_s_silu_kernel(
                     stop=(not opens and k == len(blocks) - 1),
                 )
 
-        def second_layer(e, blocks, first, width, opens, piece=None):
+        def second_layer(e, blocks, first, width, opens):
             acc = sums[e, blocks[0], first]
-            piece = piece or width
             for k, b in enumerate(blocks):
                 cols = slice(b * M, (b + 1) * M)
-                for s in range(0, width, piece):
-                    nc.tensor.matmul_mx(
-                        out=acc[:, k, s : s + piece],
-                        lhsT=wb_codes[e][:, cols].bitcast(FP8X4),
-                        lhsT_scale=wb_plane[e][:, cols],
-                        rhs=h_codes[e, first + s][:].bitcast(FP8X4),
-                        rhs_scale=h_plane[e][:, first + s : first + s + piece],
-                        start=(opens and k == 0 and s == 0),
-                        stop=(not opens and k == len(blocks) - 1 and s + piece == width),
-                    )
+                nc.tensor.matmul_mx(
+                    out=acc[:, k, :],
+                    lhsT=wb_codes[e][:, cols].bitcast(FP8X4),
+                    lhsT_scale=wb_plane[e][:, cols],
+                    rhs=h_codes[e, first][:].bitcast(FP8X4),
+                    rhs_scale=h_plane[e][:, first : first + width],
+                    start=(opens and k == 0),
+                    stop=(not opens and k == len(blocks) - 1),
+                )
 
-        def leave(e, blocks, first, width, copy, part=None, at=None):
+        def leave(e, blocks, first, width, copy, part=None, at=None, queue=None):
             acc = sums[e, blocks[0], first]
             ks = range(len(blocks)) if part is None else range(part, part + 1)
             y = made(f"y{e}_{blocks[ks[0]]}_{first}", [P, len(ks), width], F32, at)
             copy(out=y[:], in_=acc[:, ks[0] : ks[-1] + 1, :])
             rows = out[blocks[ks[0]] * M : (blocks[ks[-1]] + 1) * M, e * C + first : e * C + first + width]
-            nc.sync.dma_start(out=rows.rearrange("(b p) j -> p b j", p=P), in_=y[:])
+            (queue or nc.sync).dma_start(out=rows.rearrange("(b p) j -> p b j", p=P), in_=y[:])
 
         def leave_in_halves(e, b, copies):
             y = made(f"y{e}_{b}", [P, C], F32)
@@ -217,30 +223,39 @@ def tile_moe_elr_s_silu_kernel(
                 copy(out=y[:, s * M : (s + 1) * M], in_=sums[e, b, s * M][:, 0, :])
             nc.sync.dma_start(out=out[b * M : (b + 1) * M, e * C : (e + 1) * C], in_=y[:])
 
+        def leave_by_blocks(e, s, copies):
+            y = made(f"y{e}_s{s}", [P, 2, M], F32)
+            for b, copy in enumerate(copies):
+                copy(out=y[:, b, :], in_=sums[e, b, s * M][:, 0, :])
+            rows = out[:, e * C + s * M : e * C + (s + 1) * M]
+            nc.sync.dma_start(out=rows.rearrange("(b p) j -> p b j", p=P), in_=y[:])
+
         on_vector = nc.vector.tensor_copy
         on_scalar = nc.scalar.copy
+        sync = nc.sync
+        scalar = nc.scalar
 
         nc.sync.dma_start(offsets[:], offs)
-        load_x()
-        load_xs(nc.sync, 3)
+        load_x(sync)
+        load_xs(sync, 3)
         for r in range(3):
-            load_xs(nc.scalar, r)
-        load_was(nc.scalar, 0)
+            load_xs(scalar, r)
+        load_was(scalar, 0)
         warm_up()
-        load_was(nc.scalar, 1)
-        load_was(nc.scalar, 2)
-        load_wa(0)
-        load_wb(0)
-        load_was(nc.sync, 3)
-        load_ws(nc.sync, 0)
-        load_wa(1)
-        load_wa(2)
-        load_wb(1)
-        load_w(0, 2)
+        load_was(scalar, 1)
+        load_was(scalar, 2)
+        load_wa(sync, 0)
+        load_wb(sync, 0)
+        load_was(sync, 3)
+        load_ws(sync, 0)
+        load_wa(sync, 1)
+        load_wa(sync, 2)
+        load_wb(sync, 1)
+        load_w(sync, 0, 2)
         for r in range(1, 4):
-            load_ws(nc.sync, r)
-        load_wb(2)
-        load_w(2, 1)
+            load_ws(sync, r)
+        load_wb(sync, 2)
+        load_w(sync, 2, 1)
 
         gather_words(0, 2)
         gather_scales(0, 2)
@@ -251,25 +266,26 @@ def tile_moe_elr_s_silu_kernel(
         reorder_scales(1, 2)
         reorder_words(1, on_vector)
         reorder_words(2, on_scalar, None, slice(16, 32))
-        first_layer(0, 0, WB_AT + 1024)
-        first_layer(0, 1)
-        first_layer(1, 0)
-        first_layer(1, 1)
+        for e in range(2):
+            for s in range(2):
+                first_layer(e, s)
+                silu(e, s, WB_AT + 1024 if e == 0 else None)
         gather_words(2, 1, WAS_AT)
         gather_scales(2, 1, WAS_AT + 1024)
         reorder_words(2, on_vector, None, slice(0, 16))
         quantize_wb(0, 0, N, WAS_AT + 1280)
-        first_layer(2, 0)
-        first_layer(2, 1)
+        for s in range(2):
+            first_layer(2, s)
+            silu(2, s)
         round_wb(1, 0, N, on_vector)
         quantize_hidden(0, 0, C, "wb_bf0")
         quantize_wb(1, 0, N)
         quantize_hidden(1, 0, C, WB_AT + 1024)
-        quantize_hidden(2, 0, M)
         round_wb(2, 0, M, on_vector)
         round_wb(2, M, M, on_vector)
         quantize_wb(2, 0, M)
-        quantize_hidden(2, M, M, WB_AT + 2 * WB_BYTES)
+        quantize_hidden(2, 0, M, WB_AT + 2 * WB_BYTES)
+        quantize_hidden(2, M, M, WB_AT + 2 * WB_BYTES + 512)
         quantize_wb(2, M, M)
         bank(0, [0, 1], 0, C, psum_y, "y0")
         bank(1, [0], 0, C, psum_y, "y1")

@@ -235,6 +235,10 @@ def tile_moe_elr_s_silu_kernel(
         sync = nc.sync
         scalar = nc.scalar
 
+        def made_codes(e):
+            wa_codes[e] = made(f"wa_codes{e}", [P, H], U32)
+            return wa_codes[e]
+
         nc.sync.dma_start(offsets[:], offs)
         load_x(sync)
         load_xs(sync, 3)
@@ -260,25 +264,28 @@ def tile_moe_elr_s_silu_kernel(
         gather_words(0, 2)
         gather_scales(0, 2)
         reorder_words(0, on_scalar)
-        round_wb(0, 0, N, on_scalar, "wb_bf0")
+        round_wb(0, 0, N, on_scalar)
         reorder_scales(0, 1, slice(0, 2))
         reorder_scales(0, 1, slice(2, 4))
         reorder_scales(1, 2)
-        reorder_words(1, on_vector)
-        reorder_words(2, on_scalar, None, slice(16, 32))
+        reorder_words(1, on_vector, None, slice(0, 16))
+        reorder_words(1, on_scalar, None, slice(16, 32))
+        nc.gpsimd.tensor_copy(
+            out=made_codes(2)[:].rearrange("p (t m) -> p t m", t=PACK),
+            in_=wa_raw[2][:].rearrange("p (m t) -> p t m", t=PACK),
+        )
         for e in range(2):
             for s in range(2):
                 first_layer(e, s)
                 silu(e, s, WB_AT + 1024 if e == 0 else None)
         gather_words(2, 1, WAS_AT)
         gather_scales(2, 1, WAS_AT + 1024)
-        reorder_words(2, on_vector, None, slice(0, 16))
         quantize_wb(0, 0, N, WAS_AT + 1280)
         for s in range(2):
             first_layer(2, s)
             silu(2, s)
         round_wb(1, 0, N, on_vector)
-        quantize_hidden(0, 0, C, "wb_bf0")
+        quantize_hidden(0, 0, C, WA_AT + 2 * WA_BYTES)
         quantize_wb(1, 0, N)
         quantize_hidden(1, 0, C, WB_AT + 1024)
         round_wb(2, 0, M, on_vector)

@@ -41,10 +41,10 @@ def tile_moe_elr_s_silu_kernel(
 
         def made(name, shape, dtype, at=None):
             if at is None:
-                return keep.tile(shape, dtype, name=name, align_bytes=64)
+                return keep.tile(shape, dtype, name=name, align_bytes=256)
             if isinstance(at, str):
-                return keep.tile(shape, dtype, name=name, tag=at, align_bytes=64)
-            return shared.tile(shape, dtype, name=name, align_bytes=64, offset=at)
+                return keep.tile(shape, dtype, name=name, tag=at, align_bytes=256)
+            return shared.tile(shape, dtype, name=name, align_bytes=256, offset=at)
 
         offsets = lists.tile([P, T // 16], U16, name="offsets")
         x_window = made("x_window", [P, T], U32)

@@ -20,6 +20,7 @@ PACK = 4
 LINE = 4
 M = 128
 COLS = C // 16
+WAS_ROW = 8
 WA_BYTES = 4 * H
 WB_BYTES = 4 * PACK * N
 WAS_AT = 0
@@ -96,7 +97,7 @@ def tile_moe_elr_s_silu_kernel(
 
         def load_was(queue, r):
             rows = wa_scales[:, 0].rearrange("e b i -> b e i").bitcast(I32)
-            queue.dma_start(out=was_raw[:].bitcast(I32)[r:P:32], in_=rows[r:16:4])
+            queue.dma_start(out=was_raw[:].bitcast(I32)[WAS_ROW + r : P : 32], in_=rows[r:16:4])
 
         def load_ws(queue, r):
             rows = w_scales[:, 0].rearrange("e b n -> b e n").bitcast(I32)
@@ -157,7 +158,7 @@ def tile_moe_elr_s_silu_kernel(
                 nc.tensor.matmul_mx(
                     out=acc[:, t, :],
                     lhsT=wa_codes[e][:, cols].bitcast(FP8X4),
-                    lhsT_scale=wa_plane[:, e, cols],
+                    lhsT_scale=wa_plane[WAS_ROW:, e, cols],
                     rhs=x_codes[e][:, slots].bitcast(FP8X4),
                     rhs_scale=x_plane[e][:, slots],
                     start=True,

from contextlib import ExitStack

import concourse.mybir as mybir

K, T, E, C, H, N = 512, 768, 3, 256, 512, 256
FLOPS = 2 * E * C * (K * H + K * N + H * N)

F32 = mybir.dt.float32
BF16 = mybir.dt.bfloat16
I32 = mybir.dt.int32
U32 = mybir.dt.uint32
U16 = mybir.dt.uint16
U8 = mybir.dt.uint8
FP8X4 = mybir.dt.float8_e4m3fn_x4
FP4X4 = mybir.dt.float4_e2m1fn_x4
SILU = mybir.ActivationFunctionType.Silu

P = 128
PACK = 4
LINE = 4
M = 128
COLS = C // 16
WAS_ROW = 8
WA_BYTES = 4 * H
WB_BYTES = 4 * PACK * N
WAS_AT = 0
WA_AT = 2560
WB_AT = WA_AT + E * WA_BYTES
W_AT = WB_AT + E * WB_BYTES


def tile_moe_elr_s_silu_kernel(
    tc, x_words, x_scales, w_words, w_scales, wa_words, wa_scales, wb, offs, out
):
    nc = tc.nc
    with ExitStack() as ctx:
        lists = ctx.enter_context(tc.tile_pool(name="lists", bufs=1))
        keep = ctx.enter_context(tc.tile_pool(name="keep", bufs=1))
        shared = ctx.enter_context(tc.tile_pool(name="shared", bufs=1))
        psum_h = ctx.enter_context(tc.psum_pool(name="psum_h", bufs=4))
        psum_y = ctx.enter_context(tc.psum_pool(name="psum_y", bufs=1))

        def made(name, shape, dtype, at=None):
            if at is None:
                return keep.tile(shape, dtype, name=name, align_bytes=256)
            if isinstance(at, str):
                return keep.tile(shape, dtype, name=name, tag=at, align_bytes=256)
            return shared.tile(shape, dtype, name=name, align_bytes=256, offset=at)

        offsets = lists.tile([P, T // 16], U16, name="offsets")
        x_window = made("x_window", [P, T], U32)
        xs_window = made("xs_window", [P, T], U8)
        was_raw = made("was_raw", [P, E, H], U8, WAS_AT)
        wa_raw = [made(f"wa_raw{e}", [P, H], U32, WA_AT + e * WA_BYTES) for e in range(E)]
        wb_raw = [made(f"wb_raw{e}", [P, PACK, N], F32, WB_AT + e * WB_BYTES) for e in range(E)]
        ws_plane = made("ws_plane", [P, E, N], U8)
        wa_plane = made("wa_plane", [P, E, H], U8)
        wb_plane = [made(f"wb_plane{e}", [P, N], U8) for e in range(E)]
        h_plane = [made(f"h_plane{e}", [P, C], U8) for e in range(E)]
        w_codes = {}
        wa_codes = {}
        wb_bf = {}
        wb_codes = {}
        x_codes = {}
        x_plane = {}
        h_codes = {}
        h_bf = {}
        h_sums = {}
        sums = {}

        warm_in = keep.tile([P, 1], F32, name="warm_in")
        warm_out = keep.tile([P, 1], F32, name="warm_out")
        nc.vector.memset(xs_window[:].bitcast(I32), 0)
        nc.vector.memset(was_raw[:].rearrange("p e i -> p (e i)").bitcast(I32), 0)
        nc.vector.memset(warm_in[:], 0.0)
        nc.gpsimd.memset(ws_plane[:].rearrange("p e n -> p (e n)").bitcast(I32), 0)

        def load_x(queue):
            queue.dma_start(out=x_window[:].bitcast(I32), in_=x_words[0].rearrange("p t d -> p (t d)").bitcast(I32))

        def load_wa(queue, e):
            words = wa_words[e, 0].rearrange("p i d -> p (i d)").bitcast(I32)
            queue.dma_start(out=wa_raw[e][:].bitcast(I32), in_=words)

        def load_wb(queue, e):
            queue.dma_start(out=wb_raw[e][:], in_=wb[e].rearrange("(p j) n -> p j n", j=PACK))

        def load_w(queue, first, count, at=None):
            tile = made(f"w_codes{first}", [P, count, 2 * N], U8, at)
            words = w_words[first : first + count, 0].rearrange("e p b -> p e b").bitcast(I32)
            queue.dma_start(out=tile[:].bitcast(I32), in_=words)
            for e in range(count):
                w_codes[first + e] = tile[:, e, :]

        def load_xs(queue, r):
            queue.dma_start(out=xs_window[:].bitcast(I32)[r:P:32], in_=x_scales[0].bitcast(I32)[r:16:4])

        def load_was(queue, r):
            rows = wa_scales[:, 0].rearrange("e b i -> b e i").bitcast(I32)
            queue.dma_start(out=was_raw[:].bitcast(I32)[WAS_ROW + r : P : 32], in_=rows[r:16:4])

        def load_ws(queue, r):
            rows = w_scales[:, 0].rearrange("e b n -> b e n").bitcast(I32)
            queue.dma_start(out=ws_plane[:].bitcast(I32)[r:P:32], in_=rows[r:16:4])

        def warm_up():
            nc.scalar.activation(warm_out[:], warm_in[:], SILU)

        def gather(into, window, dtype, name, first, count, at):
            tile = made(f"{name}{first}", [P, count * C], dtype, at)
            nc.vector.tensor_copy(tile[:], window[:].indirect(offsets[:, first * COLS : (first + count) * COLS]))
            for e in range(count):
                into[first + e] = tile[:, e * C : (e + 1) * C]

        def gather_words(first, count, at=None):
            gather(x_codes, x_window, U32, "x_codes", first, count, at)

        def gather_scales(first, count, at=None):
            gather(x_plane, xs_window, U8, "x_plane", first, count, at)

        def reorder_words(e, copy, at=None, lines=slice(0, M // LINE)):
            if e not in wa_codes:
                wa_codes[e] = made(f"wa_codes{e}", [P, H], U32, at)
            copy(
                out=wa_codes[e][:].rearrange("p (t c i) -> p c t i", t=PACK, i=LINE)[:, lines],
                in_=wa_raw[e][:].rearrange("p (c i t) -> p c t i", t=PACK, i=LINE)[:, lines],
            )

        def reorder_scales(first, count, passes=slice(0, PACK)):
            experts = slice(first, first + count)
            nc.vector.tensor_copy(
                out=wa_plane[:, experts, :].rearrange("p e (t h m) -> p h e t m", t=PACK, h=2)[:, :, :, passes],
                in_=was_raw[:, experts, :].rearrange("p e (h m t) -> p h e t m", t=PACK, h=2)[:, :, :, passes],
            )

        def round_wb(e, first, width, copy, at=None):
            wb_bf[e, first] = made(f"wb_bf{e}_{first}", [P, width, PACK], BF16, at)
            copy(
                out=wb_bf[e, first][:].rearrange("p (c i) j -> p c j i", i=LINE),
                in_=wb_raw[e][:, :, first : first + width].rearrange("p j (c i) -> p c j i", i=LINE),
            )

        def quantize_wb(e, first, width, at=None):
            if e not in wb_codes:
                wb_codes[e] = made(f"wb_codes{e}", [P, N], U32, at)
            nc.vector.quantize_mx(
                out=wb_codes[e][:, first : first + width].bitcast(FP8X4),
                scales=wb_plane[e][:, first : first + width],
                in_=wb_bf[e, first][:].rearrange("p n j -> p (n j)"),
            )

        def first_layer(e, s):
            slots = slice(s * M, (s + 1) * M)
            acc = psum_h.tile([P, PACK, M], F32, name="h_acc")
            h_sums[e, s] = acc
            for t in range(PACK):
                cols = slice(t * M, (t + 1) * M)
                nc.tensor.matmul_mx(
                    out=acc[:, t, :],
                    lhsT=wa_codes[e][:, cols].bitcast(FP8X4),
                    lhsT_scale=wa_plane[WAS_ROW:, e, cols],
                    rhs=x_codes[e][:, slots].bitcast(FP8X4),
                    rhs_scale=x_plane[e][:, slots],
                    start=True,
                    stop=True,
                )

        def silu(e, s, at=None):
            if e not in h_bf:
                h_bf[e] = made(f"h_bf{e}", [P, C, PACK], BF16, at)
            nc.scalar.activation(h_bf[e][:, s * M : (s + 1) * M, :], h_sums[e, s][:].rearrange("p t u -> p u t"), SILU)

        def quantize_hidden(e, first, width, at=None):
            h_codes[e, first] = made(f"h_codes{e}_{first}", [P, width], U32, at)
            slots = slice(first, first + width)
            nc.vector.quantize_mx(
                out=h_codes[e, first][:].bitcast(FP8X4),
                scales=h_plane[e][:, slots],
                in_=h_bf[e][:, slots, :].rearrange("p u t -> p (u t)"),
            )

        def bank(e, blocks, first, width, pool, tag):
            sums[e, blocks[0], first] = pool.tile([P, len(blocks), width], F32, name="y_acc", tag=tag)

        def frozen_layer(e, blocks, first, width, opens):
            acc = sums[e, blocks[0], first]
            slots = slice(first, first + width)
            for k, b in enumerate(blocks):
                nc.tensor.matmul_mx(
                    out=acc[:, k, :],
                    lhsT=w_codes[e][:, 2 * b * M : 2 * (b + 1) * M].bitcast(FP4X4),
                    lhsT_scale=ws_plane[:, e, b * M : (b + 1) * M],
                    rhs=x_codes[e][:, slots].bitcast(FP8X4),
                    rhs_scale=x_plane[e][:, slots],
                    start=(opens and k == 0),
                    stop=(not opens and k == len(blocks) - 1),
                )

        def second_layer(e, blocks, first, width, opens):
            acc = sums[e, blocks[0], first]
            for k, b in enumerate(blocks):
                cols = slice(b * M, (b + 1) * M)
                nc.tensor.matmul_mx(
                    out=acc[:, k, :],
                    lhsT=wb_codes[e][:, cols].bitcast(FP8X4),
                    lhsT_scale=wb_plane[e][:, cols],
                    rhs=h_codes[e, first][:].bitcast(FP8X4),
                    rhs_scale=h_plane[e][:, first : first + width],
                    start=(opens and k == 0),
                    stop=(not opens and k == len(blocks) - 1),
                )

        def leave(e, blocks, first, width, copy, part=None, at=None, queue=None):
            acc = sums[e, blocks[0], first]
            ks = range(len(blocks)) if part is None else range(part, part + 1)
            y = made(f"y{e}_{blocks[ks[0]]}_{first}", [P, len(ks), width], F32, at)
            copy(out=y[:], in_=acc[:, ks[0] : ks[-1] + 1, :])
            rows = out[blocks[ks[0]] * M : (blocks[ks[-1]] + 1) * M, e * C + first : e * C + first + width]
            (queue or nc.sync).dma_start(out=rows.rearrange("(b p) j -> p b j", p=P), in_=y[:])

        def leave_in_halves(e, b, copies):
            y = made(f"y{e}_{b}", [P, C], F32)
            for s, copy in enumerate(copies):
                copy(out=y[:, s * M : (s + 1) * M], in_=sums[e, b, s * M][:, 0, :])
            nc.sync.dma_start(out=out[b * M : (b + 1) * M, e * C : (e + 1) * C], in_=y[:])

        def leave_by_blocks(e, s, copies):
            y = made(f"y{e}_s{s}", [P, 2, M], F32)
            for b, copy in enumerate(copies):
                copy(out=y[:, b, :], in_=sums[e, b, s * M][:, 0, :])
            rows = out[:, e * C + s * M : e * C + (s + 1) * M]
            nc.sync.dma_start(out=rows.rearrange("(b p) j -> p b j", p=P), in_=y[:])

        on_vector = nc.vector.tensor_copy
        on_scalar = nc.scalar.copy
        sync = nc.sync
        scalar = nc.scalar

        def made_codes(e):
            wa_codes[e] = made(f"wa_codes{e}", [P, H], U32)
            return wa_codes[e]

        nc.sync.dma_start(offsets[:], offs)
        load_x(sync)
        load_xs(sync, 3)
        for r in range(3):
            load_xs(scalar, r)
        load_was(scalar, 0)
        warm_up()
        load_was(scalar, 1)
        load_was(scalar, 2)
        load_wa(sync, 0)
        load_wb(sync, 0)
        load_was(sync, 3)
        load_ws(sync, 0)
        load_wa(sync, 1)
        load_wa(sync, 2)
        load_wb(sync, 1)
        load_w(sync, 0, 2)
        for r in range(1, 4):
            load_ws(sync, r)
        load_wb(sync, 2)
        load_w(sync, 2, 1)

        gather_words(0, 2)
        gather_scales(0, 2)
        reorder_words(0, on_scalar)
        round_wb(0, 0, N, on_scalar)
        reorder_scales(0, 1, slice(0, 2))
        reorder_scales(0, 1, slice(2, 4))
        reorder_scales(1, 2)
        reorder_words(1, on_vector, None, slice(0, 16))
        reorder_words(1, on_scalar, None, slice(16, 32))
        nc.gpsimd.tensor_copy(
            out=made_codes(2)[:].rearrange("p (t m) -> p t m", t=PACK),
            in_=wa_raw[2][:].rearrange("p (m t) -> p t m", t=PACK),
        )
        for e in range(2):
            for s in range(2):
                first_layer(e, s)
                silu(e, s, WB_AT + 1024 if e == 0 else None)
        gather_words(2, 1, WAS_AT)
        gather_scales(2, 1, WAS_AT + 1024)
        quantize_wb(0, 0, N, WAS_AT + 1280)
        for s in range(2):
            first_layer(2, s)
            silu(2, s)
        round_wb(1, 0, N, on_vector)
        quantize_hidden(0, 0, C, WA_AT + 2 * WA_BYTES)
        quantize_wb(1, 0, N)
        quantize_hidden(1, 0, C, WB_AT + 1024)
        round_wb(2, 0, M, on_vector)
        round_wb(2, M, M, on_vector)
        quantize_wb(2, 0, M)
        quantize_hidden(2, 0, M, WB_AT + 2 * WB_BYTES)
        quantize_hidden(2, M, M, WB_AT + 2 * WB_BYTES + 512)
        quantize_wb(2, M, M)
        bank(0, [0, 1], 0, C, psum_y, "y0")
        bank(1, [0], 0, C, psum_y, "y1")
        bank(1, [1], 0, C, psum_h, "h_acc")
        bank(2, [0], 0, M, psum_h, "h_acc")
        bank(2, [0], M, M, psum_h, "h_acc")
        bank(2, [1], 0, M, psum_y, "y2")
        bank(2, [1], M, M, psum_y, "y3")
        second_layer(0, [0, 1], 0, C, True)
        frozen_layer(0, [0, 1], 0, C, False)
        frozen_layer(1, [0], 0, C, True)
        frozen_layer(1, [1], 0, C, True)
        second_layer(1, [0], 0, C, False)
        second_layer(1, [1], 0, C, False)
        for b in range(2):
            for s in range(0, C, M):
                frozen_layer(2, [b], s, M, True)
        for b in range(2):
            for s in range(0, C, M):
                second_layer(2, [b], s, M, False)
        leave(0, [0, 1], 0, C, on_scalar, 0)
        leave(0, [0, 1], 0, C, on_scalar, 1)
        leave(1, [0], 0, C, on_scalar)
        leave(1, [1], 0, C, on_scalar)
        leave_in_halves(2, 0, [on_scalar, on_vector])
        leave_in_halves(2, 1, [on_scalar, on_vector])
